import numpy as np
import ml_dtypes


def mxq(x, axis, fmt="e4m3"):
    dtype, down = {"e4m3": (ml_dtypes.float8_e4m3fn, 7), "e5m2": (ml_dtypes.float8_e5m2, 14)}[fmt]
    v = np.moveaxis(np.asarray(x, np.float32).astype(ml_dtypes.bfloat16).astype(np.float64), axis, -1)
    blocks = v.reshape(v.shape[:-1] + (-1, 32))
    amax = np.abs(blocks).max(-1, keepdims=True)
    byte = np.maximum(np.where(amax > 0, np.frexp(amax)[1] - 1 + 127, 0) - down, 1)
    scale = np.exp2(byte - 127.0)
    codes = (blocks / scale).astype(np.float32).astype(dtype).astype(np.float64)
    return np.moveaxis((codes * scale).reshape(v.shape), -1, axis)


WIDE = False


def mx_kscale(k):
    if not WIDE:
        return np.ones(k)
    levels = np.array([10, -10, 5, -5, 0])
    if k % 512:
        return np.exp2(np.random.permutation(np.resize(levels, k // 32))).repeat(32)
    a = np.empty((k // 512, 16))
    for p in range(k // 512):
        a[p, :8] = np.random.permutation(np.resize(levels, 8))
        for g in range(8):
            far = levels[np.abs(levels - a[p, g]) >= 10]
            a[p, g + 8] = far[np.random.randint(len(far))]
    return np.exp2(a.ravel()).repeat(32)


BF16 = ml_dtypes.bfloat16


def bf(x):
    return np.asarray(x, np.float32).astype(BF16)


def f64(x):
    return np.asarray(x).astype(np.float64)

def planes(Y):
    n, m = Y.shape
    b = f64(bf(Y)).reshape(n // 32, 32, m)
    amax = np.abs(b).max(1)
    byte = np.clip(np.where(amax > 0, np.frexp(amax)[1] - 1 + 127 - 7, 1), 1, 254)
    codes = (b * np.exp2(127.0 - byte)[:, None, :]).reshape(n, m).astype(np.float32).astype(ml_dtypes.float8_e4m3fn).view(np.uint8)
    words = codes.reshape(n // 512, 128, 4, m).transpose(0, 1, 3, 2)
    return np.ascontiguousarray(words), np.ascontiguousarray(byte.astype(np.uint8).reshape(n // 512, 16, m))


NI, NT, KI, KT, N = 1024, 2048, 1536, 1024, 1024


def noise(*shape):
    return np.random.standard_normal(shape)

def setup_inputs():
    s = mx_kscale(KI)
    t = mx_kscale(KT)
    spread = np.exp(0.6 * noise(N))
    return {
        "image": bf(noise(NI, KI) * s),
        "w_image": bf(noise(KI, N) / np.sqrt(KI) * spread / s[:, None]),
        "b_image": bf(0.3 * noise(N) * spread),
        "text": bf(noise(NT, KT) * t),
        "w_text": bf(noise(KT, N) / np.sqrt(KT) / t[:, None]),
        "b_text": bf(0.3 * noise(N)),
        "g_text": bf(np.exp(0.8 * noise(N))),
    }

def reference(image, w_image, b_image, text, w_text, b_text, g_text):
    xi = mxq(f64(image), 1, "e4m3")
    wi = mxq(f64(w_image), 0, "e4m3")
    u = (xi @ wi) + f64(b_image)
    xt = mxq(f64(text), 1, "e4m3")
    wt = mxq(f64(w_text), 0, "e4m3")
    v = np.tanh((xt @ wt) + f64(b_text)) * f64(g_text)
    y = np.concatenate([u, v], axis=0)
    Y = y.T
    words, scales = planes(Y)
    return y, words, scales

@@ -1,0 +1,483 @@
+from contextlib import ExitStack
+
+import concourse.mybir as mybir
+from concourse.masks import make_identity
+
+NI, NT, KI, KT, N = 1024, 2048, 1536, 1024, 1024
+FLOPS = 2 * (NI * KI + NT * KT) * N
+
+F32 = mybir.dt.float32
+BF16 = mybir.dt.bfloat16
+I32 = mybir.dt.int32
+U32 = mybir.dt.uint32
+U8 = mybir.dt.uint8
+FP8X4 = mybir.dt.float8_e4m3fn_x4
+ALU = mybir.AluOpType
+ACT = mybir.ActivationFunctionType
+
+P = 128
+PACK = 4
+KP = 512
+HALF = 512
+IMG_ROWS = 256
+TXT_ROWS = 512
+IMG_PASSES = KI // KP
+TXT_PASSES = KT // KP
+
+HEAD_V_COLS = 320
+IMG_V_COLS = 128
+TXT_V_COLS = 512
+Y_ON_V = ()
+CAST_ON_S = [(b, g) for b in range(4) for g in range(2)]
+ORDER = [("t", 0, 0), ("t", 1, 0), ("t", 0, 1), ("t", 1, 1), ("t", 2, 0), ("t", 2, 1), ("t", 3, 0), ("t", 3, 1)] + [("i", b, g) for g in range(2) for b in range(4)]
+A_PLAN = (2,3,4,5, 6,7,8,9, 10,11,12, 13,14,15, 16,16,16, 17,17,17)
+W_PLAN = (1,2,5,7,9,11,13,15)
+XB = 4
+XBT = 3
+XR = 5
+WR = 5
+YB = 4
+YBF = 3
+BIAS_AT = 2
+LATE_IL = 1
+WARM = (0, 0, 0)
+
+
+def tile_contrastive_two_tower_embeddings_g1_kernel(
+    tc, image, w_image, b_image, text, w_text, b_text, g_text, out_0, out_1, out_2
+):
+    nc = tc.nc
+    words_out = out_1.rearrange("g p m t -> g p (m t)").bitcast(I32)
+    scales_out = out_2.bitcast(I32)
+
+    rounds = []
+    for tower, b, g in ORDER:
+        rounds += [("img", b, g)] if tower == "i" else [("txt", b, g, 0), ("txt", b, g, 1)]
+    n_rounds = len(rounds)
+    first_use = {}
+    for r, rd in enumerate(rounds):
+        first_use.setdefault(("x", rd[0], rd[1]), r)
+        first_use.setdefault(("w", rd[0], rd[2]), r)
+    act_jobs, w_jobs = [], []
+    for key, r in first_use.items():
+        if key[0] == "x" and key[1] == "img":
+            act_jobs += [("img", key[2], c, 0) for c in range(IMG_PASSES)]
+        elif key[0] == "x":
+            act_jobs += [("txt", key[2], c, h) for c in range(TXT_PASSES) for h in range(2)]
+        else:
+            passes = IMG_PASSES if key[1] == "img" else TXT_PASSES
+            w_jobs += [(key[1], c, key[2]) for c in range(passes)]
+    act_plan, w_plan = {}, {}
+    for job, at in zip(act_jobs[8:], A_PLAN):
+        assert at + 2 <= first_use[("x",) + job[:2]]
+        act_plan.setdefault(at, []).append(job)
+    for job, at in zip(w_jobs[2:], W_PLAN):
+        assert at + 2 <= first_use[("w", job[0], job[2])]
+        w_plan.setdefault(at, []).append(job)
+
+    with ExitStack() as ctx:
+        keep = ctx.enter_context(tc.tile_pool(name="keep", bufs=1))
+        work = ctx.enter_context(tc.tile_pool(name="work", bufs=2))
+        psum = ctx.enter_context(tc.psum_pool(name="psum", bufs=8))
+        ctx.enter_context(tc.manual_schedule())
+
+        ident = keep.tile([P, P], F32, name="ident")
+        make_identity(nc, ident[:])
+
+        w_codes = {
+            "img": keep.tile([P, IMG_PASSES, N], U32, name="wi_codes", align_bytes=64),
+            "txt": keep.tile([P, TXT_PASSES, N], U32, name="wt_codes", align_bytes=64),
+        }
+        w_scales = {
+            "img": keep.tile([P, IMG_PASSES, N], U8, name="wi_scales", align_bytes=64),
+            "txt": keep.tile([P, TXT_PASSES, N], U8, name="wt_scales", align_bytes=64),
+        }
+        y_scales, scales_left = {}, {}
+        for tower, rows in (("img", NI), ("txt", NT)):
+            for g in range(2):
+                y_scales[tower, g] = keep.tile([P, rows], U8, name="y_scales_%s%d" % (tower, g), align_bytes=64)
+                scales_left[tower, g] = rows
+        bt = keep.tile([P, 2, PACK], BF16, name="bt")
+        gt = keep.tile([P, 2, PACK], BF16, name="gt")
+        bi = keep.tile([P, 2, PACK], BF16, name="bi")
+        bi_rows = keep.tile([P, N], BF16, name="bi_rows")
+
+        x_raw, x_grouped, x_codes, x_scales = {}, {}, {}, {}
+        w_raw, w_grouped = {}, {}
+        v_t, y_rows, y_bf, y_grouped = {}, {}, {}, {}
+
+        def bank():
+            return psum.tile([P, 512], F32, name="bank", tag="bank")
+
+        def load_w(job):
+            tower, c, g = job
+            w = w_image if tower == "img" else w_text
+            raw = work.tile([P, PACK, HALF], BF16, name="w_raw", tag="w_raw", bufs=WR)
+            nc.sync.dma_start(
+                out=raw[:],
+                in_=w[c * KP : (c + 1) * KP, g * HALF : (g + 1) * HALF].rearrange("(p j) n -> p j n", j=PACK),
+            )
+            w_raw[job] = raw
+
+        def load_x(tower, b, c0, c1):
+            x, rows = (image, IMG_ROWS) if tower == "img" else (text, TXT_ROWS)
+            raw = work.tile([P, rows // P, (c1 - c0) * KP], BF16, name="x_raw", tag="x_raw", bufs=XR)
+            nc.sync.dma_start(
+                out=raw[:],
+                in_=x[b * rows : (b + 1) * rows, c0 * KP : c1 * KP].rearrange("(i p) k -> p i k", p=P),
+            )
+            for c in range(c0, c1):
+                x_raw[tower, b, c] = raw[:, :, (c - c0) * KP : (c - c0 + 1) * KP].bitcast(F32)
+
+        def interleave_w(job, copy, lo, hi):
+            if lo == hi:
+                return
+            if job not in w_grouped:
+                w_grouped[job] = work.tile([P, PACK * HALF], BF16, name="w_grouped", tag="w_grouped", bufs=3, align_bytes=64)
+            raw, grouped = w_raw[job][:, :, lo:hi], w_grouped[job]
+            if job[0] == "img":
+                dst = grouped[:, PACK * lo : PACK * hi].rearrange("p (c i j) -> p c j i", i=4, j=PACK)
+                copy(out=dst, in_=raw.rearrange("p j (c i) -> p c j i", i=4))
+            else:
+                dst = grouped[:].rearrange("p (t m j) -> p m j t", t=PACK, j=PACK)[:, lo // PACK : hi // PACK]
+                copy(out=dst, in_=raw.rearrange("p j (m t) -> p m j t", t=PACK))
+
+        def quantize_w(job):
+            tower, c, g = job
+            cols = slice(g * HALF, (g + 1) * HALF)
+            nc.vector.quantize_mx(
+                out=w_codes[tower][:, c, cols].bitcast(FP8X4), scales=w_scales[tower][:, c, cols], in_=w_grouped[job][:]
+            )
+
+        def turn_x(job, copy=nc.scalar.copy):
+            tower, b, c, h = job
+            rows = IMG_ROWS if tower == "img" else TXT_ROWS
+            ps = bank()
+            for i in range(2):
+                for u in range(2):
+                    nc.tensor.transpose(
+                        ps[:, (2 * i + u) * P : (2 * i + u + 1) * P], x_raw[tower, b, c][:, 2 * h + i, u::2], ident[:]
+                    )
+            if h == 0:
+                x_grouped[tower, b, c] = work.tile(
+                    [P, PACK * rows], BF16, name="x_grouped", tag="x_grouped", bufs=4, align_bytes=64
+                )
+            dst = x_grouped[tower, b, c][:].bitcast(F32)[:, h * 512 : (h + 1) * 512]
+            copy(
+                out=dst.rearrange("p (i r u) -> p i r u", i=2, u=2),
+                in_=ps[:].rearrange("p (i u r) -> p i r u", i=2, u=2),
+            )
+
+        def quantize_x(job):
+            tower, b, c, h = job
+            rows = IMG_ROWS if tower == "img" else TXT_ROWS
+            if h != rows // 256 - 1:
+                return
+            nb = XB * IMG_PASSES if tower == "img" else XBT * TXT_PASSES
+            codes = work.tile([P, rows], U32, name="x_codes", tag="x_codes_" + tower, bufs=nb, align_bytes=64)
+            scales = work.tile([P, rows], U8, name="x_scales", tag="x_scales_" + tower, bufs=nb, align_bytes=64)
+            nc.vector.quantize_mx(out=codes[:].bitcast(FP8X4), scales=scales[:], in_=x_grouped[tower, b, c][:])
+            x_codes[tower, b, c], x_scales[tower, b, c] = codes, scales
+
+        def mx_pass(rd, s, c, ps):
+            tower, b, g = rd[:3]
+            passes = IMG_PASSES if tower == "img" else TXT_PASSES
+            xc, xs = x_codes[tower, b, c], x_scales[tower, b, c]
+            wc, ws = w_codes[tower][:, c, :], w_scales[tower][:, c, :]
+            if tower == "img":
+                still = slice(s * P, (s + 1) * P)
+                moving = slice(g * HALF, (g + 1) * HALF)
+                lhs, lhs_s, rhs, rhs_s = xc[:, still], xs[:, still], wc[:, moving], ws[:, moving]
+            else:
+                t = 2 * rd[3] + s
+                still = slice(g * HALF + t * P, g * HALF + (t + 1) * P)
+                lhs, lhs_s, rhs, rhs_s = wc[:, still], ws[:, still], xc[:], xs[:]
+            nc.tensor.matmul_mx(
+                out=ps[:],
+                lhsT=lhs.bitcast(FP8X4),
+                lhsT_scale=lhs_s,
+                rhs=rhs.bitcast(FP8X4),
+                rhs_scale=rhs_s,
+                start=(c == 0),
+                stop=(c == passes - 1),
+            )
+
+        def product(rd, s):
+            ps = bank()
+            for c in range(IMG_PASSES if rd[0] == "img" else TXT_PASSES):
+                mx_pass(rd, s, c, ps)
+            return ps
+
+        def add_bias(unit, s, ps):
+            g = unit[2]
+            if s == 0:
+                y_rows[unit] = work.tile([P, 2, HALF], F32, name="y_rows", tag="y_rows", bufs=YB)
+            nc.vector.tensor_tensor(
+                out=y_rows[unit][:, s, :], in0=ps[:], in1=bi_rows[:, g * HALF : (g + 1) * HALF], op=ALU.add
+            )
+
+        def squash(rd, s, ps):
+            unit, g, t = rd[:3], rd[2], 2 * rd[3] + s
+            if t == 0:
+                v_t[unit] = work.tile([P, PACK, TXT_ROWS], F32, name="v_t", tag="v_t", bufs=3)
+            nc.scalar.activation(out=v_t[unit][:, t, :], in_=ps[:], func=ACT.Tanh, bias=bt[:, g, t : t + 1])
+
+        def gain(rd):
+            unit, g = rd[:3], rd[2]
+            for t in (2 * rd[3], 2 * rd[3] + 1):
+                nc.vector.tensor_scalar(
+                    out=v_t[unit][:, t, :], in0=v_t[unit][:, t, :], scalar1=gt[:, g, t : t + 1], scalar2=None, op0=ALU.mult
+                )
+
+        def row0(unit):
+            return unit[1] * IMG_ROWS if unit[0] == "img" else NI + unit[1] * TXT_ROWS
+
+        def store_y(unit):
+            tower, b, g = unit
+            rows = IMG_ROWS if tower == "img" else TXT_ROWS
+            dst = out_0[row0(unit) : row0(unit) + rows, g * HALF : (g + 1) * HALF]
+            nc.sync.dma_start(out=dst.rearrange("(i p) n -> p i n", p=P), in_=y_rows[unit][:])
+
+        def round_to_bf16(unit):
+            if unit[0] == "img":
+                y_bf[unit] = work.tile([P, 2 * HALF], BF16, name="y_bf", tag="y_bf", bufs=YBF)
+                copy = nc.scalar.copy if unit[1:] in CAST_ON_S else nc.vector.tensor_copy
+                copy(
+                    out=y_bf[unit][:].rearrange("r (i u p e) -> r i p u e", i=2, u=2, e=2),
+                    in_=y_rows[unit][:].rearrange("r i (p u e) -> r i p u e", u=2, e=2),
+                )
+            else:
+                y_grouped[unit] = work.tile(
+                    [P, PACK * TXT_ROWS], BF16, name="y_grouped", tag="y_grouped", bufs=3, align_bytes=64
+                )
+                nc.vector.tensor_copy(
+                    out=y_grouped[unit][:].rearrange("p (c i t) -> p c t i", i=4, t=PACK),
+                    in_=v_t[unit][:].rearrange("p t (c i) -> p c t i", i=4),
+                )
+
+        def turn_y_words(unit):
+            ps = bank()
+            words = y_bf[unit][:].bitcast(F32)
+            for q in range(4):
+                nc.tensor.transpose(ps[:, q * P : (q + 1) * P], words[:, q * P : (q + 1) * P], ident[:])
+            y_grouped[unit] = work.tile(
+                [P, PACK * IMG_ROWS], BF16, name="y_grouped", tag="y_grouped", bufs=3, align_bytes=64
+            )
+            nc.scalar.copy(
+                out=y_grouped[unit][:].bitcast(F32).rearrange("p (i r u) -> p i r u", i=2, u=2),
+                in_=ps[:].rearrange("p (i u r) -> p i r u", i=2, u=2),
+            )
+
+        def turn_v(unit, i):
+            ps = bank()
+            for t in range(PACK):
+                nc.tensor.transpose(ps[:, t * P : (t + 1) * P], v_t[unit][:, t, i * P : (i + 1) * P], ident[:])
+            if i == 0:
+                y_rows[unit] = work.tile([P, 4, HALF], F32, name="y_rows", tag="y_rows", bufs=YB)
+            copy = nc.vector.tensor_copy if (2 * unit[1] + unit[2], i) in Y_ON_V else nc.scalar.copy
+            copy(
+                out=y_rows[unit][:, i, :].rearrange("r (p t) -> r p t", t=PACK),
+                in_=ps[:].rearrange("r (t p) -> r p t", t=PACK),
+            )
+            if i == 3:
+                store_y(unit)
+
+        def quantize_y(unit):
+            tower, b, g = unit
+            rows = IMG_ROWS if tower == "img" else TXT_ROWS
+            m0 = row0(unit)
+            codes = work.tile([P, rows], U32, name="y_codes", tag="y_codes", bufs=3, align_bytes=64)
+            nc.vector.quantize_mx(
+                out=codes[:].bitcast(FP8X4),
+                scales=y_scales[tower, g][:, b * rows : (b + 1) * rows],
+                in_=y_grouped[unit][:],
+            )
+            nc.sync.dma_start(out=words_out[g, :, m0 : m0 + rows], in_=codes[:].bitcast(I32))
+            scales_left[tower, g] -= rows
+            if scales_left[tower, g] == 0:
+                lo, hi = (0, NI) if tower == "img" else (NI, NI + NT)
+                for q in range(4):
+                    queue = nc.scalar if (sum(scales_left.values()) == 0 and q % 2) else nc.sync
+                    queue.dma_start(
+                        out=scales_out[g, 4 * q : 4 * q + 4, lo // 4 : hi // 4],
+                        in_=y_scales[tower, g][32 * q : 32 * q + 4, :].bitcast(I32),
+                    )
+
+        def spread_bias():
+            ps = bank()
+            words = bi[:].rearrange("p g t -> p (g t)").bitcast(F32)
+            for q in range(4):
+                nc.tensor.transpose(ps[:, q * P : (q + 1) * P], words[:, q : q + 1].to_broadcast([P, P]), ident[:])
+            nc.scalar.copy(
+                out=bi_rows[:].bitcast(F32).rearrange("r (g p u) -> r g p u", g=2, u=2),
+                in_=ps[:].rearrange("r (g u p) -> r g p u", g=2, u=2),
+            )
+
+        loads = []
+        for r in range(n_rounds):
+            loads += [("w", job) for job in w_plan.get(r, [])]
+            loads += [("x", job) for job in act_plan.get(r, []) if job[2:] == (0, 0)]
+        free = {"x": XR - 4, "w": WR - 2}
+
+        def issue_loads():
+            while loads and free[loads[0][0]] > 0:
+                kind, job = loads[0]
+                loads.remove(loads[0])
+                free[kind] -= 1
+                if kind == "w":
+                    load_w(job)
+                else:
+                    load_x(job[0], job[1], 0, IMG_PASSES if job[0] == "img" else TXT_PASSES)
+
+        def warm(n):
+            if n:
+                ps = bank()
+            for k in range(n):
+                nc.tensor.matmul_mx(
+                    out=ps[:, :P],
+                    lhsT=warm_codes[:, :P].bitcast(FP8X4),
+                    lhsT_scale=warm_scales[:, :P],
+                    rhs=warm_codes[:].bitcast(FP8X4),
+                    rhs_scale=warm_scales[:],
+                    start=True,
+                    stop=True,
+                )
+
+        def prepare_head_w(job):
+            interleave_w(job, nc.vector.tensor_copy, 0, HEAD_V_COLS)
+            interleave_w(job, nc.scalar.copy, HEAD_V_COLS, HALF)
+
+        if sum(WARM):
+            warm_in = work.tile([P, PACK * P], BF16, name="warm_in", tag="w_grouped", bufs=3, align_bytes=64)
+            warm_codes = keep.tile([P, P], U32, name="warm_codes", align_bytes=64)
+            warm_scales = keep.tile([P, P], U8, name="warm_scales", align_bytes=64)
+            nc.vector.memset(warm_in[:], 0.0)
+            nc.vector.quantize_mx(out=warm_codes[:].bitcast(FP8X4), scales=warm_scales[:], in_=warm_in[:])
+        load_x("txt", 0, 0, 1)
+        load_w(("txt", 0, 0))
+        load_x("txt", 0, 1, 2)
+        load_x("txt", 1, 0, 1)
+        load_w(("txt", 1, 0))
+        load_x("txt", 1, 1, 2)
+        nc.sync.dma_start(out=bt[:], in_=b_text.rearrange("(g p t) -> p g t", g=2, t=PACK))
+        nc.sync.dma_start(out=gt[:], in_=g_text.rearrange("(g p t) -> p g t", g=2, t=PACK))
+        issue_loads()
+        nc.sync.dma_start(out=bi[:], in_=b_image.rearrange("(g p t) -> p g t", g=2, t=PACK))
+        warm(WARM[0])
+        turn_x(("txt", 0, 0, 0))
+        turn_x(("txt", 0, 0, 1), nc.vector.tensor_copy)
+        prepare_head_w(("txt", 0, 0))
+        quantize_x(("txt", 0, 0, 1))
+        quantize_w(("txt", 0, 0))
+        warm(WARM[1])
+        turn_x(("txt", 0, 1, 0))
+        turn_x(("txt", 0, 1, 1))
+        warm(WARM[2])
+        first = [(rounds[t // 2], t % 2, bank()) for t in range(PACK)]
+        for rd, s, ps in first:
+            mx_pass(rd, s, 0, ps)
+        quantize_x(("txt", 0, 1, 1))
+        prepare_head_w(("txt", 1, 0))
+        turn_x(("txt", 1, 0, 0))
+        turn_x(("txt", 1, 0, 1))
+        quantize_w(("txt", 1, 0))
+        quantize_x(("txt", 1, 0, 1))
+        turn_x(("txt", 1, 1, 0))
+        turn_x(("txt", 1, 1, 1))
+        free["x"] += 4
+        free["w"] += 2
+        issue_loads()
+        for rd, s, ps in first:
+            mx_pass(rd, s, 1, ps)
+            squash(rd, s, ps)
+        quantize_x(("txt", 1, 1, 1))
+        for job in w_plan.get(1, []):
+            interleave_w(job, nc.vector.tensor_copy, 0, HALF)
+            free["w"] += 1
+        gain(rounds[0])
+
+        def done(r):
+            if 0 <= r < n_rounds and (rounds[r][0] == "img" or rounds[r][3] == 1):
+                return rounds[r][:3]
+            return None
+
+        last = n_rounds - 1
+        for r in range(2, n_rounds):
+            rd = rounds[r]
+            one, two, three = done(r - 1), done(r - 2), done(r - 3)
+            w_now = w_plan.get(r, [])
+            v_cols = IMG_V_COLS if rd[0] == "img" else TXT_V_COLS
+            if rounds[r - 1][0] == "txt":
+                gain(rounds[r - 1])
+            if rd[0] == "img":
+                for job in w_now:
+                    interleave_w(job, nc.scalar.copy, v_cols, (v_cols + HALF) // 2)
+            if one and one[0] == "img" and one[1:] in CAST_ON_S:
+                round_to_bf16(one)
+            for job in w_plan.get(r - 1, []):
+                quantize_w(job)
+            if two and two[0] == "txt" and r - 2 > LATE_IL:
+                quantize_y(two)
+            if three and (three[0] == "img" or r - 3 <= LATE_IL):
+                quantize_y(three)
+            if one and (one[0] == "img" and one[1:] not in CAST_ON_S or one[0] == "txt" and r - 1 > LATE_IL):
+                round_to_bf16(one)
+            if two and two[0] == "txt" and r - 2 <= LATE_IL:
+                round_to_bf16(two)
+            for job in w_now:
+                interleave_w(job, nc.vector.tensor_copy, 0, v_cols)
+            if r == last:
+                break
+            for s in range(2):
+                ps = product(rd, s)
+                if rd[0] == "img":
+                    add_bias(rd, s, ps)
+                else:
+                    squash(rd, s, ps)
+            if rd[0] == "img":
+                store_y(rd)
+            for job in act_plan.get(r - 1, []):
+                quantize_x(job)
+            if r == BIAS_AT:
+                spread_bias()
+            if two and two[0] == "img":
+                turn_y_words(two)
+            if one and one[0] == "txt":
+                turn_v(one, 0)
+                turn_v(one, 1)
+            if two and two[0] == "txt":
+                turn_v(two, 2)
+                turn_v(two, 3)
+            for job in act_plan.get(r, []):
+                turn_x(job)
+                if job[2:] == ((IMG_PASSES - 1, 0) if job[0] == "img" else (TXT_PASSES - 1, 1)):
+                    free["x"] += 1
+            for job in w_now:
+                lo = (v_cols + HALF) // 2 if rd[0] == "img" else v_cols
+                interleave_w(job, nc.scalar.copy, lo, HALF)
+                free["w"] += 1
+            issue_loads()
+
+        unit, g = rounds[last], rounds[last][2]
+        turn_y_words(rounds[last - 2])
+        y_bf[unit] = work.tile([P, 2 * HALF], BF16, name="y_bf", tag="y_bf", bufs=YBF)
+        bias = bi_rows[:, g * HALF : (g + 1) * HALF]
+        banks = []
+        for s in range(2):
+            ps = product(unit, s)
+            banks.append(ps)
+            nc.vector.tensor_tensor(
+                out=y_bf[unit][:, s * HALF : (s + 1) * HALF].rearrange("r (u p e) -> r u p e", u=2, e=2),
+                in0=ps[:].rearrange("r (p u e) -> r u p e", u=2, e=2),
+                in1=bias.rearrange("r (p u e) -> r u p e", u=2, e=2),
+                op=ALU.add,
+            )
+            if s == 0:
+                add_bias(unit, s, ps)
+                quantize_y(rounds[last - 2])
+        turn_y_words(rounds[last - 1])
+        turn_y_words(unit)
+        add_bias(unit, 1, banks[1])
+        store_y(unit)
+        quantize_y(rounds[last - 1])
+        quantize_y(unit)

@@ -17,30 +17,24 @@ ACT = mybir.ActivationFunctionType
 
 P = 128
 PACK = 4
-KP = 512
-HALF = 512
-IMG_ROWS = 256
-TXT_ROWS = 512
-IMG_PASSES = KI // KP
-TXT_PASSES = KT // KP
+KP = P * PACK
+BANK = 512
+ROWS = {"img": 256, "txt": 512}
+PASSES = {"img": KI // KP, "txt": KT // KP}
+TXT_ROUNDS = 16
+ROUNDS = 24
 
 HEAD_V_COLS = 320
-IMG_V_COLS = 128
-TXT_V_COLS = 512
-Y_ON_V = ()
-CAST_ON_S = [(b, g) for b in range(4) for g in range(2)]
-ORDER = [("t", 0, 0), ("t", 1, 0), ("t", 0, 1), ("t", 1, 1), ("t", 2, 0), ("t", 2, 1), ("t", 3, 0), ("t", 3, 1)] + [("i", b, g) for g in range(2) for b in range(4)]
-A_PLAN = (2,3,4,5, 6,7,8,9, 10,11,12, 13,14,15, 16,16,16, 17,17,17)
-W_PLAN = (1,2,5,7,9,11,13,15)
-XB = 4
-XBT = 3
-XR = 5
-WR = 5
-YB = 4
-YBF = 3
-BIAS_AT = 2
-LATE_IL = 1
 WARM = (0, 0, 0)
+SLOTS = 15
+LEAD = 4
+IL_AT = {11: 17, 13: 18, 15: 19}
+A_PLAN = (1,1,2,2,3,4,5,6,6,7,8,9,10,11,12,13,14,15,16,17,18,19,20,20)
+W_PLAN = (2, 6, 10, 13, 14, 15)
+Y_ON_V = [(h, 3) for h in range(5)]
+CAST_ON_V = ()
+MXB = 8
+YG = 3
 
 
 def tile_contrastive_two_tower_embeddings_g1_kernel(
@@ -49,31 +43,30 @@ def tile_contrastive_two_tower_embeddings_g1_kernel(
     nc = tc.nc
     words_out = out_1.rearrange("g p m t -> g p (m t)").bitcast(I32)
     scales_out = out_2.bitcast(I32)
+    x_in = {"img": image, "txt": text}
+    w_in = {"img": w_image, "txt": w_text}
+    first_row = {"img": 0, "txt": NI}
 
-    rounds = []
-    for tower, b, g in ORDER:
-        rounds += [("img", b, g)] if tower == "i" else [("txt", b, g, 0), ("txt", b, g, 1)]
-    n_rounds = len(rounds)
-    first_use = {}
-    for r, rd in enumerate(rounds):
-        first_use.setdefault(("x", rd[0], rd[1]), r)
-        first_use.setdefault(("w", rd[0], rd[2]), r)
-    act_jobs, w_jobs = [], []
-    for key, r in first_use.items():
-        if key[0] == "x" and key[1] == "img":
-            act_jobs += [("img", key[2], c, 0) for c in range(IMG_PASSES)]
-        elif key[0] == "x":
-            act_jobs += [("txt", key[2], c, h) for c in range(TXT_PASSES) for h in range(2)]
-        else:
-            passes = IMG_PASSES if key[1] == "img" else TXT_PASSES
-            w_jobs += [(key[1], c, key[2]) for c in range(passes)]
-    act_plan, w_plan = {}, {}
-    for job, at in zip(act_jobs[8:], A_PLAN):
-        assert at + 2 <= first_use[("x",) + job[:2]]
-        act_plan.setdefault(at, []).append(job)
-    for job, at in zip(w_jobs[2:], W_PLAN):
-        assert at + 2 <= first_use[("w", job[0], job[2])]
+    def unit_of(r):
+        if r < TXT_ROUNDS:
+            return ("txt", r // 4, r // 2 % 2)
+        return ("img", (r - TXT_ROUNDS) // 2, r % 2)
+
+    def ended(tower, r):
+        if 0 <= r < ROUNDS and unit_of(r)[0] == tower and (tower == "img" or r % 2 == 1):
+            return unit_of(r)
+        return None
+
+    x_jobs = [("txt", b, c, h) for b in range(1, 4) for c in range(2) for h in range(2)]
+    x_jobs += [("img", b, c, 0) for b in range(4) for c in range(3)]
+    x_plan, w_plan = {}, {}
+    for job, at in zip(x_jobs, A_PLAN):
+        x_plan.setdefault(at, []).append(job)
+    for job, at in zip([("img", c, g) for c in range(3) for g in range(2)], W_PLAN):
         w_plan.setdefault(at, []).append(job)
+
+    def needed(job):
+        return 4 * job[1] if job[0] == "txt" else TXT_ROUNDS + 2 * job[1]
 
     with ExitStack() as ctx:
         keep = ctx.enter_context(tc.tile_pool(name="keep", bufs=1))
@@ -84,19 +77,11 @@ def tile_contrastive_two_tower_embeddings_g1_kernel(
         ident = keep.tile([P, P], F32, name="ident")
         make_identity(nc, ident[:])
 
-        w_codes = {
-            "img": keep.tile([P, IMG_PASSES, N], U32, name="wi_codes", align_bytes=64),
-            "txt": keep.tile([P, TXT_PASSES, N], U32, name="wt_codes", align_bytes=64),
-        }
-        w_scales = {
-            "img": keep.tile([P, IMG_PASSES, N], U8, name="wi_scales", align_bytes=64),
-            "txt": keep.tile([P, TXT_PASSES, N], U8, name="wt_scales", align_bytes=64),
-        }
-        y_scales, scales_left = {}, {}
+        w_codes, w_scales, y_scales = {}, {}, {}
         for tower, rows in (("img", NI), ("txt", NT)):
-            for g in range(2):
-                y_scales[tower, g] = keep.tile([P, rows], U8, name="y_scales_%s%d" % (tower, g), align_bytes=64)
-                scales_left[tower, g] = rows
+            w_codes[tower] = keep.tile([P, PASSES[tower], N], U32, name="w_codes_" + tower, align_bytes=64)
+            w_scales[tower] = keep.tile([P, PASSES[tower], N], U8, name="w_scales_" + tower, align_bytes=64)
+            y_scales[tower] = keep.tile([P, 2, rows], U8, name="y_scales_" + tower, align_bytes=64)
         bt = keep.tile([P, 2, PACK], BF16, name="bt")
         gt = keep.tile([P, 2, PACK], BF16, name="gt")
         bi = keep.tile([P, 2, PACK], BF16, name="bi")
@@ -106,91 +91,102 @@ def tile_contrastive_two_tower_embeddings_g1_kernel(
         w_raw, w_grouped = {}, {}
         v_t, y_rows, y_bf, y_grouped = {}, {}, {}, {}
 
-        def bank():
-            return psum.tile([P, 512], F32, name="bank", tag="bank")
+        spare = list(range(SLOTS))
+        slot_of = {}
 
-        def load_w(job):
-            tower, c, g = job
-            w = w_image if tower == "img" else w_text
-            raw = work.tile([P, PACK, HALF], BF16, name="w_raw", tag="w_raw", bufs=WR)
-            nc.sync.dma_start(
-                out=raw[:],
-                in_=w[c * KP : (c + 1) * KP, g * HALF : (g + 1) * HALF].rearrange("(p j) n -> p j n", j=PACK),
-            )
-            w_raw[job] = raw
+        def take(key, shape, dtype):
+            slot_of[key] = spare[0]
+            spare.remove(spare[0])
+            return work.tile(shape, dtype, name="big", tag="slot%d" % slot_of[key], bufs=1)
 
-        def load_x(tower, b, c0, c1):
-            x, rows = (image, IMG_ROWS) if tower == "img" else (text, TXT_ROWS)
-            raw = work.tile([P, rows // P, (c1 - c0) * KP], BF16, name="x_raw", tag="x_raw", bufs=XR)
-            nc.sync.dma_start(
-                out=raw[:],
-                in_=x[b * rows : (b + 1) * rows, c0 * KP : c1 * KP].rearrange("(i p) k -> p i k", p=P),
-            )
-            for c in range(c0, c1):
-                x_raw[tower, b, c] = raw[:, :, (c - c0) * KP : (c - c0 + 1) * KP].bitcast(F32)
+        def give(key):
+            spare.append(slot_of[key])
+
+        def bank(kind):
+            if MXB == 8:
+                return psum.tile([P, BANK], F32, name="bank", tag="bank", bufs=8)
+            return psum.tile([P, BANK], F32, name="bank", tag=kind, bufs=MXB if kind == "mx" else 8 - MXB)
+
+        def half(g):
+            return slice(g * KP, (g + 1) * KP)
+
+        def load_vector(tile, vector):
+            nc.sync.dma_start(out=tile[:], in_=vector.rearrange("(g p t) -> p g t", g=2, t=PACK))
+
+        def load_w(tower, c, halves):
+            cols = slice(halves[0] * KP, (halves[-1] + 1) * KP)
+            raw = take(("w", tower, c, halves[-1]), [P, PACK, len(halves) * KP], BF16)
+            nc.sync.dma_start(out=raw[:], in_=w_in[tower][half(c), cols].rearrange("(p j) n -> p j n", j=PACK))
+            for g in halves:
+                w_raw[tower, c, g] = raw[:, :, half(g - halves[0])]
+
+        def load_x(tower, b, pairs):
+            rows = ROWS[tower]
+            src = x_in[tower][b * rows : (b + 1) * rows, :].rearrange("(p i) k -> p i k" if tower == "txt" else "(i p) k -> p i k", p=P)
+            src = src[:, 2 * pairs[0] : 2 * pairs[-1] + 2, :]
+            raw = take(("x", tower, b, pairs[-1]), list(src.shape), BF16)
+            nc.sync.dma_start(out=raw[:], in_=src)
+            for h in pairs:
+                x_raw[tower, b, h] = raw[:, 2 * (h - pairs[0]) : 2 * (h - pairs[0]) + 2, :].bitcast(F32)
 
         def interleave_w(job, copy, lo, hi):
-            if lo == hi:
-                return
+            tower, c, g = job
             if job not in w_grouped:
-                w_grouped[job] = work.tile([P, PACK * HALF], BF16, name="w_grouped", tag="w_grouped", bufs=3, align_bytes=64)
+                w_grouped[job] = work.tile([P, PACK * KP], BF16, name="w_grouped", tag="w_grouped", bufs=3, align_bytes=64)
             raw, grouped = w_raw[job][:, :, lo:hi], w_grouped[job]
-            if job[0] == "img":
-                dst = grouped[:, PACK * lo : PACK * hi].rearrange("p (c i j) -> p c j i", i=4, j=PACK)
-                copy(out=dst, in_=raw.rearrange("p j (c i) -> p c j i", i=4))
+            if tower == "img":
+                dst = grouped[:, PACK * lo : PACK * hi].rearrange("p (a i j) -> p a j i", i=4, j=PACK)
+                copy(out=dst, in_=raw.rearrange("p j (a i) -> p a j i", i=4))
             else:
-                dst = grouped[:].rearrange("p (t m j) -> p m j t", t=PACK, j=PACK)[:, lo // PACK : hi // PACK]
-                copy(out=dst, in_=raw.rearrange("p j (m t) -> p m j t", t=PACK))
+                dst = grouped[:].rearrange("p (t a b j) -> p a t b j", t=PACK, b=2, j=PACK)[:, lo // 8 : hi // 8]
+                copy(out=dst, in_=raw.rearrange("p j (a b t) -> p a t b j", b=2, t=PACK))
 
         def quantize_w(job):
             tower, c, g = job
-            cols = slice(g * HALF, (g + 1) * HALF)
             nc.vector.quantize_mx(
-                out=w_codes[tower][:, c, cols].bitcast(FP8X4), scales=w_scales[tower][:, c, cols], in_=w_grouped[job][:]
+                out=w_codes[tower][:, c, half(g)].bitcast(FP8X4),
+                scales=w_scales[tower][:, c, half(g)],
+                in_=w_grouped[job][:],
             )
 
-        def turn_x(job, copy=nc.scalar.copy):
+        def turn_x(job):
             tower, b, c, h = job
-            rows = IMG_ROWS if tower == "img" else TXT_ROWS
-            ps = bank()
+            ps = bank("turn")
             for i in range(2):
                 for u in range(2):
-                    nc.tensor.transpose(
-                        ps[:, (2 * i + u) * P : (2 * i + u + 1) * P], x_raw[tower, b, c][:, 2 * h + i, u::2], ident[:]
-                    )
+                    words = x_raw[tower, b, h][:, i, c * 256 + u : (c + 1) * 256 : 2]
+                    nc.tensor.transpose(ps[:, (2 * i + u) * P : (2 * i + u + 1) * P], words, ident[:])
             if h == 0:
                 x_grouped[tower, b, c] = work.tile(
-                    [P, PACK * rows], BF16, name="x_grouped", tag="x_grouped", bufs=4, align_bytes=64
+                    [P, PACK * ROWS[tower]], BF16, name="x_grouped", tag="x_grouped", bufs=4, align_bytes=64
                 )
-            dst = x_grouped[tower, b, c][:].bitcast(F32)[:, h * 512 : (h + 1) * 512]
-            copy(
-                out=dst.rearrange("p (i r u) -> p i r u", i=2, u=2),
-                in_=ps[:].rearrange("p (i u r) -> p i r u", i=2, u=2),
-            )
+            dst = x_grouped[tower, b, c][:].bitcast(F32)
+            if tower == "img":
+                dst = dst.rearrange("p (i r u) -> p i r u", i=2, u=2)
+                src = ps[:].rearrange("p (i u r) -> p i r u", i=2, u=2)
+            else:
+                dst = dst.rearrange("p (r i u) -> p r i u", i=4, u=2)[:, :, 2 * h : 2 * h + 2, :]
+                src = ps[:].rearrange("p (i u r) -> p r i u", i=2, u=2)
+            return lambda: nc.scalar.copy(out=dst, in_=src)
 
         def quantize_x(job):
             tower, b, c, h = job
-            rows = IMG_ROWS if tower == "img" else TXT_ROWS
-            if h != rows // 256 - 1:
+            if tower == "txt" and h == 0:
                 return
-            nb = XB * IMG_PASSES if tower == "img" else XBT * TXT_PASSES
-            codes = work.tile([P, rows], U32, name="x_codes", tag="x_codes_" + tower, bufs=nb, align_bytes=64)
-            scales = work.tile([P, rows], U8, name="x_scales", tag="x_scales_" + tower, bufs=nb, align_bytes=64)
+            bufs = 9 if tower == "img" else 4
+            codes = work.tile([P, ROWS[tower]], U32, name="x_codes", tag="x_codes_" + tower, bufs=bufs, align_bytes=64)
+            scales = work.tile([P, ROWS[tower]], U8, name="x_scales", tag="x_scales_" + tower, bufs=bufs, align_bytes=64)
             nc.vector.quantize_mx(out=codes[:].bitcast(FP8X4), scales=scales[:], in_=x_grouped[tower, b, c][:])
             x_codes[tower, b, c], x_scales[tower, b, c] = codes, scales
 
-        def mx_pass(rd, s, c, ps):
-            tower, b, g = rd[:3]
-            passes = IMG_PASSES if tower == "img" else TXT_PASSES
+        def mx_pass(unit, s, c, ps):
+            tower, b, g = unit
             xc, xs = x_codes[tower, b, c], x_scales[tower, b, c]
-            wc, ws = w_codes[tower][:, c, :], w_scales[tower][:, c, :]
+            wc, ws = w_codes[tower][:, c, half(g)], w_scales[tower][:, c, half(g)]
+            still = slice(s * P, (s + 1) * P)
             if tower == "img":
-                still = slice(s * P, (s + 1) * P)
-                moving = slice(g * HALF, (g + 1) * HALF)
-                lhs, lhs_s, rhs, rhs_s = xc[:, still], xs[:, still], wc[:, moving], ws[:, moving]
+                lhs, lhs_s, rhs, rhs_s = xc[:, still], xs[:, still], wc, ws
             else:
-                t = 2 * rd[3] + s
-                still = slice(g * HALF + t * P, g * HALF + (t + 1) * P)
                 lhs, lhs_s, rhs, rhs_s = wc[:, still], ws[:, still], xc[:], xs[:]
             nc.tensor.matmul_mx(
                 out=ps[:],
@@ -199,112 +195,108 @@ def tile_contrastive_two_tower_embeddings_g1_kernel(
                 rhs=rhs.bitcast(FP8X4),
                 rhs_scale=rhs_s,
                 start=(c == 0),
-                stop=(c == passes - 1),
+                stop=(c == PASSES[tower] - 1),
             )
 
-        def product(rd, s):
-            ps = bank()
-            for c in range(IMG_PASSES if rd[0] == "img" else TXT_PASSES):
-                mx_pass(rd, s, c, ps)
+        def product(unit, s):
+            ps = bank("mx")
+            for c in range(PASSES[unit[0]]):
+                mx_pass(unit, s, c, ps)
             return ps
 
+        def y_tile(key):
+            if key not in y_rows:
+                y_rows[key] = take(("y",) + key, [P, 2, N], F32)
+            return y_rows[key]
+
         def add_bias(unit, s, ps):
-            g = unit[2]
-            if s == 0:
-                y_rows[unit] = work.tile([P, 2, HALF], F32, name="y_rows", tag="y_rows", bufs=YB)
-            nc.vector.tensor_tensor(
-                out=y_rows[unit][:, s, :], in0=ps[:], in1=bi_rows[:, g * HALF : (g + 1) * HALF], op=ALU.add
+            tower, b, g = unit
+            nc.vector.tensor_tensor(out=y_tile((tower, b))[:, s, half(g)], in0=ps[:], in1=bi_rows[:, half(g)], op=ALU.add)
+
+        def image_rows(b):
+            return out_0[b * ROWS["img"] : (b + 1) * ROWS["img"], :].rearrange("(i r) n -> r i n", i=2)
+
+        def squash(unit, t, ps):
+            if unit not in v_t:
+                v_t[unit] = take(("v", unit), [P, PACK, ROWS["txt"]], F32)
+            nc.scalar.activation(out=v_t[unit][:, t, :], in_=ps[:], func=ACT.Tanh, bias=bt[:, unit[2], t : t + 1])
+
+        def gain(r):
+            unit = unit_of(r)
+            for t in (2 * (r % 2), 2 * (r % 2) + 1):
+                v = v_t[unit][:, t, :]
+                nc.vector.tensor_scalar(out=v, in0=v, scalar1=gt[:, unit[2], t : t + 1], scalar2=None, op0=ALU.mult)
+
+        def grouped_tile(unit):
+            y_grouped[unit] = work.tile(
+                [P, PACK * ROWS[unit[0]]], BF16, name="y_grouped", tag="y_grouped", bufs=YG, align_bytes=64
+            )
+            return y_grouped[unit]
+
+        def round_v(unit):
+            nc.vector.tensor_copy(
+                out=grouped_tile(unit)[:].rearrange("p (a i t) -> p a t i", i=4, t=PACK),
+                in_=v_t[unit][:].rearrange("p t (a i) -> p a t i", i=4),
             )
 
-        def squash(rd, s, ps):
-            unit, g, t = rd[:3], rd[2], 2 * rd[3] + s
-            if t == 0:
-                v_t[unit] = work.tile([P, PACK, TXT_ROWS], F32, name="v_t", tag="v_t", bufs=3)
-            nc.scalar.activation(out=v_t[unit][:, t, :], in_=ps[:], func=ACT.Tanh, bias=bt[:, g, t : t + 1])
-
-        def gain(rd):
-            unit, g = rd[:3], rd[2]
-            for t in (2 * rd[3], 2 * rd[3] + 1):
-                nc.vector.tensor_scalar(
-                    out=v_t[unit][:, t, :], in0=v_t[unit][:, t, :], scalar1=gt[:, g, t : t + 1], scalar2=None, op0=ALU.mult
-                )
-
-        def row0(unit):
-            return unit[1] * IMG_ROWS if unit[0] == "img" else NI + unit[1] * TXT_ROWS
-
-        def store_y(unit):
+        def round_u(unit):
             tower, b, g = unit
-            rows = IMG_ROWS if tower == "img" else TXT_ROWS
-            dst = out_0[row0(unit) : row0(unit) + rows, g * HALF : (g + 1) * HALF]
-            nc.sync.dma_start(out=dst.rearrange("(i p) n -> p i n", p=P), in_=y_rows[unit][:])
+            y_bf[unit] = work.tile([P, 2 * KP], BF16, name="y_bf", tag="y_bf", bufs=3)
+            copy = nc.vector.tensor_copy if unit[1:] in CAST_ON_V else nc.scalar.copy
+            copy(
+                out=y_bf[unit][:].rearrange("r (i u p e) -> r i u p e", i=2, u=2, e=2),
+                in_=y_rows[tower, b][:, :, half(g)].rearrange("r i (p u e) -> r i u p e", u=2, e=2),
+            )
 
-        def round_to_bf16(unit):
-            if unit[0] == "img":
-                y_bf[unit] = work.tile([P, 2 * HALF], BF16, name="y_bf", tag="y_bf", bufs=YBF)
-                copy = nc.scalar.copy if unit[1:] in CAST_ON_S else nc.vector.tensor_copy
-                copy(
-                    out=y_bf[unit][:].rearrange("r (i u p e) -> r i p u e", i=2, u=2, e=2),
-                    in_=y_rows[unit][:].rearrange("r i (p u e) -> r i p u e", u=2, e=2),
-                )
-            else:
-                y_grouped[unit] = work.tile(
-                    [P, PACK * TXT_ROWS], BF16, name="y_grouped", tag="y_grouped", bufs=3, align_bytes=64
-                )
-                nc.vector.tensor_copy(
-                    out=y_grouped[unit][:].rearrange("p (c i t) -> p c t i", i=4, t=PACK),
-                    in_=v_t[unit][:].rearrange("p t (c i) -> p c t i", i=4),
-                )
-
-        def turn_y_words(unit):
-            ps = bank()
+        def turn_u(unit):
+            ps = bank("turn")
             words = y_bf[unit][:].bitcast(F32)
             for q in range(4):
                 nc.tensor.transpose(ps[:, q * P : (q + 1) * P], words[:, q * P : (q + 1) * P], ident[:])
-            y_grouped[unit] = work.tile(
-                [P, PACK * IMG_ROWS], BF16, name="y_grouped", tag="y_grouped", bufs=3, align_bytes=64
-            )
             nc.scalar.copy(
-                out=y_grouped[unit][:].bitcast(F32).rearrange("p (i r u) -> p i r u", i=2, u=2),
+                out=grouped_tile(unit)[:].bitcast(F32).rearrange("p (i r u) -> p i r u", i=2, u=2),
                 in_=ps[:].rearrange("p (i u r) -> p i r u", i=2, u=2),
             )
 
         def turn_v(unit, i):
-            ps = bank()
+            tower, b, g = unit
+            ps = bank("turn")
             for t in range(PACK):
                 nc.tensor.transpose(ps[:, t * P : (t + 1) * P], v_t[unit][:, t, i * P : (i + 1) * P], ident[:])
-            if i == 0:
-                y_rows[unit] = work.tile([P, 4, HALF], F32, name="y_rows", tag="y_rows", bufs=YB)
-            copy = nc.vector.tensor_copy if (2 * unit[1] + unit[2], i) in Y_ON_V else nc.scalar.copy
-            copy(
-                out=y_rows[unit][:, i, :].rearrange("r (p t) -> r p t", t=PACK),
-                in_=ps[:].rearrange("r (t p) -> r p t", t=PACK),
+            dst = y_tile((tower, b, i // 2))[:, i % 2, half(g)]
+            copy = nc.vector.tensor_copy if (2 * b + g, i) in Y_ON_V else nc.scalar.copy
+            return lambda: copy(
+                out=dst.rearrange("r (p t) -> r p t", t=PACK), in_=ps[:].rearrange("r (t p) -> r p t", t=PACK)
             )
-            if i == 3:
-                store_y(unit)
+
+        def store_v(b, pair):
+            m0 = NI + b * ROWS["txt"] + pair * 2 * P
+            dst = out_0[m0 : m0 + 2 * P, :].rearrange("(i r) n -> r i n", i=2)
+            nc.sync.dma_start(out=dst, in_=y_rows["txt", b, pair][:])
+            give(("y", "txt", b, pair))
+
+        def store_scales(tower, queues):
+            lo, rows = first_row[tower], y_scales[tower].shape[2]
+            for q in range(4):
+                queues[q % len(queues)].dma_start(
+                    out=scales_out[:, 4 * q : 4 * q + 4, lo // 4 : (lo + rows) // 4].rearrange("g r m -> r g m"),
+                    in_=y_scales[tower][32 * q : 32 * q + 4, :, :].bitcast(I32),
+                )
 
         def quantize_y(unit):
             tower, b, g = unit
-            rows = IMG_ROWS if tower == "img" else TXT_ROWS
-            m0 = row0(unit)
-            codes = work.tile([P, rows], U32, name="y_codes", tag="y_codes", bufs=3, align_bytes=64)
+            rows = ROWS[tower]
+            m0 = first_row[tower] + b * rows
+            codes = work.tile([P, rows], U32, name="y_codes", tag="y_codes", bufs=4, align_bytes=64)
             nc.vector.quantize_mx(
                 out=codes[:].bitcast(FP8X4),
-                scales=y_scales[tower, g][:, b * rows : (b + 1) * rows],
+                scales=y_scales[tower][:, g, b * rows : (b + 1) * rows],
                 in_=y_grouped[unit][:],
             )
             nc.sync.dma_start(out=words_out[g, :, m0 : m0 + rows], in_=codes[:].bitcast(I32))
-            scales_left[tower, g] -= rows
-            if scales_left[tower, g] == 0:
-                lo, hi = (0, NI) if tower == "img" else (NI, NI + NT)
-                for q in range(4):
-                    queue = nc.scalar if (sum(scales_left.values()) == 0 and q % 2) else nc.sync
-                    queue.dma_start(
-                        out=scales_out[g, 4 * q : 4 * q + 4, lo // 4 : hi // 4],
-                        in_=y_scales[tower, g][32 * q : 32 * q + 4, :].bitcast(I32),
-                    )
 
         def spread_bias():
-            ps = bank()
+            ps = bank("turn")
             words = bi[:].rearrange("p g t -> p (g t)").bitcast(F32)
             for q in range(4):
                 nc.tensor.transpose(ps[:, q * P : (q + 1) * P], words[:, q : q + 1].to_broadcast([P, P]), ident[:])
@@ -314,170 +306,182 @@ def tile_contrastive_two_tower_embeddings_g1_kernel(
             )
 
         loads = []
-        for r in range(n_rounds):
-            loads += [("w", job) for job in w_plan.get(r, [])]
-            loads += [("x", job) for job in act_plan.get(r, []) if job[2:] == (0, 0)]
-        free = {"x": XR - 4, "w": WR - 2}
+        for r in range(ROUNDS):
+            loads += [(r, "w", job) for job in w_plan.get(r, []) if job[2] == 0]
+            loads += [(r, "x", job) for job in x_plan.get(r, []) if job[2:] == (0, 0)]
 
-        def issue_loads():
-            while loads and free[loads[0][0]] > 0:
-                kind, job = loads[0]
+        def issue_loads(now):
+            while loads and loads[0][0] <= now + LEAD:
+                r, kind, job = loads[0]
                 loads.remove(loads[0])
-                free[kind] -= 1
                 if kind == "w":
-                    load_w(job)
+                    load_w(job[0], job[1], (0, 1))
                 else:
-                    load_x(job[0], job[1], 0, IMG_PASSES if job[0] == "img" else TXT_PASSES)
+                    load_x(job[0], job[1], (0,) if job[0] == "img" else (0, 1))
+
+        warm_codes = keep.tile([P, P], U32, name="warm_codes", align_bytes=64)
+        warm_scales = keep.tile([P, P], U8, name="warm_scales", align_bytes=64)
 
         def warm(n):
-            if n:
-                ps = bank()
+            if n == 0:
+                return
+            ps = bank("turn")
             for k in range(n):
                 nc.tensor.matmul_mx(
                     out=ps[:, :P],
-                    lhsT=warm_codes[:, :P].bitcast(FP8X4),
-                    lhsT_scale=warm_scales[:, :P],
+                    lhsT=warm_codes[:].bitcast(FP8X4),
+                    lhsT_scale=warm_scales[:],
                     rhs=warm_codes[:].bitcast(FP8X4),
                     rhs_scale=warm_scales[:],
                     start=True,
                     stop=True,
                 )
 
-        def prepare_head_w(job):
+        def share_w(job):
             interleave_w(job, nc.vector.tensor_copy, 0, HEAD_V_COLS)
-            interleave_w(job, nc.scalar.copy, HEAD_V_COLS, HALF)
+            interleave_w(job, nc.scalar.copy, HEAD_V_COLS, KP)
 
         if sum(WARM):
-            warm_in = work.tile([P, PACK * P], BF16, name="warm_in", tag="w_grouped", bufs=3, align_bytes=64)
-            warm_codes = keep.tile([P, P], U32, name="warm_codes", align_bytes=64)
-            warm_scales = keep.tile([P, P], U8, name="warm_scales", align_bytes=64)
+            warm_in = work.tile([P, KP], BF16, name="warm_in", tag="w_grouped", bufs=3, align_bytes=64)
             nc.vector.memset(warm_in[:], 0.0)
             nc.vector.quantize_mx(out=warm_codes[:].bitcast(FP8X4), scales=warm_scales[:], in_=warm_in[:])
-        load_x("txt", 0, 0, 1)
-        load_w(("txt", 0, 0))
-        load_x("txt", 0, 1, 2)
-        load_x("txt", 1, 0, 1)
-        load_w(("txt", 1, 0))
-        load_x("txt", 1, 1, 2)
-        nc.sync.dma_start(out=bt[:], in_=b_text.rearrange("(g p t) -> p g t", g=2, t=PACK))
-        nc.sync.dma_start(out=gt[:], in_=g_text.rearrange("(g p t) -> p g t", g=2, t=PACK))
-        issue_loads()
-        nc.sync.dma_start(out=bi[:], in_=b_image.rearrange("(g p t) -> p g t", g=2, t=PACK))
+        load_vector(bi, b_image)
+        for k in range(2):
+            load_x("txt", 0, (k,))
+            load_w("txt", k, (0,))
+        for c in range(2):
+            load_w("txt", c, (1,))
+        load_vector(bt, b_text)
+        load_vector(gt, g_text)
         warm(WARM[0])
-        turn_x(("txt", 0, 0, 0))
-        turn_x(("txt", 0, 0, 1), nc.vector.tensor_copy)
-        prepare_head_w(("txt", 0, 0))
-        quantize_x(("txt", 0, 0, 1))
+        spread_bias()
+        for c in range(2):
+            turn_x(("txt", 0, c, 0))()
+        share_w(("txt", 0, 0))
         quantize_w(("txt", 0, 0))
         warm(WARM[1])
-        turn_x(("txt", 0, 1, 0))
-        turn_x(("txt", 0, 1, 1))
+        for c in range(2):
+            turn_x(("txt", 0, c, 1))()
+        issue_loads(1)
         warm(WARM[2])
-        first = [(rounds[t // 2], t % 2, bank()) for t in range(PACK)]
-        for rd, s, ps in first:
-            mx_pass(rd, s, 0, ps)
-        quantize_x(("txt", 0, 1, 1))
-        prepare_head_w(("txt", 1, 0))
-        turn_x(("txt", 1, 0, 0))
-        turn_x(("txt", 1, 0, 1))
+        share_w(("txt", 1, 0))
+        for c in range(2):
+            quantize_x(("txt", 0, c, 1))
         quantize_w(("txt", 1, 0))
-        quantize_x(("txt", 1, 0, 1))
-        turn_x(("txt", 1, 1, 0))
-        turn_x(("txt", 1, 1, 1))
-        free["x"] += 4
-        free["w"] += 2
-        issue_loads()
-        for rd, s, ps in first:
-            mx_pass(rd, s, 1, ps)
-            squash(rd, s, ps)
-        quantize_x(("txt", 1, 1, 1))
-        for job in w_plan.get(1, []):
-            interleave_w(job, nc.vector.tensor_copy, 0, HALF)
-            free["w"] += 1
-        gain(rounds[0])
+        share_w(("txt", 0, 1))
+        quantize_w(("txt", 0, 1))
+        share_w(("txt", 1, 1))
+        for k in range(2):
+            give(("x", "txt", 0, k))
+            give(("w", "txt", k, 0))
+            give(("w", "txt", k, 1))
+        first = [bank("mx" if t < MXB else "turn") for t in range(PACK)]
+        for c in range(2):
+            for t in range(PACK):
+                mx_pass(unit_of(0), t, c, first[t])
+        for t in range(PACK):
+            squash(unit_of(0), t, first[t])
+        quantize_w(("txt", 1, 1))
+        gain(0)
+        for job in x_plan[1]:
+            turn_x(job)()
 
-        def done(r):
-            if 0 <= r < n_rounds and (rounds[r][0] == "img" or rounds[r][3] == 1):
-                return rounds[r][:3]
-            return None
-
-        last = n_rounds - 1
-        for r in range(2, n_rounds):
-            rd = rounds[r]
-            one, two, three = done(r - 1), done(r - 2), done(r - 3)
-            w_now = w_plan.get(r, [])
-            v_cols = IMG_V_COLS if rd[0] == "img" else TXT_V_COLS
-            if rounds[r - 1][0] == "txt":
-                gain(rounds[r - 1])
-            if rd[0] == "img":
-                for job in w_now:
-                    interleave_w(job, nc.scalar.copy, v_cols, (v_cols + HALF) // 2)
-            if one and one[0] == "img" and one[1:] in CAST_ON_S:
-                round_to_bf16(one)
+        last = ROUNDS - 1
+        for r in range(2, last):
+            unit = unit_of(r)
+            lagged = [job for job in x_plan.get(r - 2, []) if r - 1 < TXT_ROUNDS and r < needed(job) and r > 2]
+            prompt = [job for job in x_plan.get(r - 1, []) if not (r < TXT_ROUNDS and r + 1 < needed(job))]
+            if r - 1 < TXT_ROUNDS:
+                gain(r - 1)
+            for job in lagged:
+                quantize_x(job)
+            if ended("img", r - 1):
+                round_u(ended("img", r - 1))
+                if unit[2] == 0:
+                    give(("y",) + ended("img", r - 1)[:2])
             for job in w_plan.get(r - 1, []):
                 quantize_w(job)
-            if two and two[0] == "txt" and r - 2 > LATE_IL:
-                quantize_y(two)
-            if three and (three[0] == "img" or r - 3 <= LATE_IL):
-                quantize_y(three)
-            if one and (one[0] == "img" and one[1:] not in CAST_ON_S or one[0] == "txt" and r - 1 > LATE_IL):
-                round_to_bf16(one)
-            if two and two[0] == "txt" and r - 2 <= LATE_IL:
-                round_to_bf16(two)
-            for job in w_now:
-                interleave_w(job, nc.vector.tensor_copy, 0, v_cols)
-            if r == last:
-                break
-            for s in range(2):
-                ps = product(rd, s)
-                if rd[0] == "img":
-                    add_bias(rd, s, ps)
-                else:
-                    squash(rd, s, ps)
-            if rd[0] == "img":
-                store_y(rd)
-            for job in act_plan.get(r - 1, []):
-                quantize_x(job)
-            if r == BIAS_AT:
-                spread_bias()
-            if two and two[0] == "img":
-                turn_y_words(two)
-            if one and one[0] == "txt":
-                turn_v(one, 0)
-                turn_v(one, 1)
-            if two and two[0] == "txt":
-                turn_v(two, 2)
-                turn_v(two, 3)
-            for job in act_plan.get(r, []):
-                turn_x(job)
-                if job[2:] == ((IMG_PASSES - 1, 0) if job[0] == "img" else (TXT_PASSES - 1, 1)):
-                    free["x"] += 1
-            for job in w_now:
-                lo = (v_cols + HALF) // 2 if rd[0] == "img" else v_cols
-                interleave_w(job, nc.scalar.copy, lo, HALF)
-                free["w"] += 1
-            issue_loads()
+            for q in range(1, TXT_ROUNDS, 2):
+                if IL_AT.get(q, q + 2) == r - 1:
+                    quantize_y(unit_of(q))
+            if ended("img", r - 3):
+                quantize_y(ended("img", r - 3))
+            if max(IL_AT.get(q, q + 2) for q in range(1, TXT_ROUNDS, 2)) == r - 1:
+                store_scales("txt", [nc.sync])
+            if unit[0] == "txt":
+                for job in prompt:
+                    quantize_x(job)
+            for q in range(1, TXT_ROUNDS, 2):
+                if IL_AT.get(q, q + 2) == r and unit[0] == "txt":
+                    round_v(unit_of(q))
+                if max(IL_AT.get(q, q + 2), q + 3) == r - 1:
+                    give(("v", unit_of(q)))
+            for job in w_plan.get(r, []):
+                interleave_w(job, nc.vector.tensor_copy, 0, KP)
+                if job[2] == 1:
+                    give(("w", job[0], job[1], 1))
+            if unit[0] == "txt":
+                banks = [product(unit, 2 * (r % 2) + s) for s in range(2)]
+                for s in (1, 0):
+                    squash(unit, 2 * (r % 2) + s, banks[s])
+            else:
+                add_bias(unit, 0, product(unit, 0))
+                for job in prompt:
+                    quantize_x(job)
+                add_bias(unit, 1, product(unit, 1))
+                for q in range(1, TXT_ROUNDS, 2):
+                    if IL_AT.get(q, q + 2) == r:
+                        round_v(unit_of(q))
+                if unit[2] == 1:
+                    nc.sync.dma_start(out=image_rows(unit[1]), in_=y_rows[unit[:2]][:])
+                elif r == last - 1:
+                    nc.sync.dma_start(out=image_rows(unit[1])[:, :, half(0)], in_=y_rows[unit[:2]][:, :, half(0)])
+            copies = []
+            for job in x_plan.get(r, []):
+                copies.append(turn_x(job))
+                if job[2:] == ((2, 0) if job[0] == "img" else (1, 1)):
+                    give(("x", job[0], job[1], job[3]))
+            for pair in range(2):
+                source = ended("txt", r - 2 - pair)
+                if source:
+                    copies += [turn_v(source, 2 * pair), turn_v(source, 2 * pair + 1)]
+            for copy in reversed(copies) if unit[0] == "txt" else copies:
+                copy()
+            for pair in range(2):
+                source = ended("txt", r - 2 - pair)
+                if source and source[2] == 1:
+                    store_v(source[1], pair)
+            if ended("img", r - 2):
+                turn_u(ended("img", r - 2))
+            issue_loads(r)
 
-        unit, g = rounds[last], rounds[last][2]
-        turn_y_words(rounds[last - 2])
-        y_bf[unit] = work.tile([P, 2 * HALF], BF16, name="y_bf", tag="y_bf", bufs=YBF)
-        bias = bi_rows[:, g * HALF : (g + 1) * HALF]
-        banks = []
+        unit = unit_of(last)
+        tower, b, g = unit
+        turn_u(unit_of(last - 2))
+        round_u(unit_of(last - 1))
+        quantize_y(unit_of(last - 3))
+        y_bf[unit] = work.tile([P, 2 * KP], BF16, name="y_bf", tag="y_bf", bufs=3)
+        quantize_y(unit_of(last - 2))
+        banks = [product(unit, s) for s in range(2)]
         for s in range(2):
-            ps = product(unit, s)
-            banks.append(ps)
             nc.vector.tensor_tensor(
-                out=y_bf[unit][:, s * HALF : (s + 1) * HALF].rearrange("r (u p e) -> r u p e", u=2, e=2),
-                in0=ps[:].rearrange("r (p u e) -> r u p e", u=2, e=2),
-                in1=bias.rearrange("r (p u e) -> r u p e", u=2, e=2),
+                out=y_bf[unit][:, half(s)].rearrange("r (u p e) -> r u p e", u=2, e=2),
+                in0=banks[s][:].rearrange("r (p u e) -> r u p e", u=2, e=2),
+                in1=bi_rows[:, half(g)].rearrange("r (p u e) -> r u p e", u=2, e=2),
                 op=ALU.add,
             )
-            if s == 0:
-                add_bias(unit, s, ps)
-                quantize_y(rounds[last - 2])
-        turn_y_words(rounds[last - 1])
-        turn_y_words(unit)
-        add_bias(unit, 1, banks[1])
-        store_y(unit)
-        quantize_y(rounds[last - 1])
+            add_bias(unit, s, banks[s])
+            nc.sync.dma_start(out=image_rows(b)[:, s, half(g)], in_=y_rows[tower, b][:, s, half(g)])
+        turn_u(unit_of(last - 1))
+        words, grouped = y_bf[unit][:].bitcast(F32), grouped_tile(unit)[:].bitcast(F32)
+        for s in range(2):
+            ps = bank("turn")
+            for u in range(2):
+                nc.tensor.transpose(ps[:, u * P : (u + 1) * P], words[:, (2 * s + u) * P : (2 * s + u + 1) * P], ident[:])
+            nc.scalar.copy(
+                out=grouped[:, 2 * s * P : 2 * (s + 1) * P].rearrange("p (r u) -> p r u", u=2),
+                in_=ps[:, : 2 * P].rearrange("p (u r) -> p r u", u=2),
+            )
+        quantize_y(unit_of(last - 1))
         quantize_y(unit)
+        store_scales("img", [nc.sync, nc.scalar])

@@ -17,24 +17,23 @@ ACT = mybir.ActivationFunctionType
 
 P = 128
 PACK = 4
-KP = P * PACK
-BANK = 512
+SPAN = P * PACK
+PAIRS = SPAN // 2
+HALVES = N // SPAN
 ROWS = {"img": 256, "txt": 512}
-PASSES = {"img": KI // KP, "txt": KT // KP}
-TXT_ROUNDS = 16
-ROUNDS = 24
+PASSES = {"img": KI // SPAN, "txt": KT // SPAN}
+BLOCKS = 4
+TEXT_UNITS = BLOCKS * HALVES
+TEXT_ROUNDS = 2 * TEXT_UNITS
+ROUNDS = TEXT_ROUNDS + BLOCKS * HALVES
 
-HEAD_V_COLS = 320
-WARM = (0, 0, 0)
-SLOTS = 15
-LEAD = 4
-IL_AT = {11: 17, 13: 18, 15: 19}
-A_PLAN = (1,1,2,2,3,4,5,6,6,7,8,9,10,11,12,13,14,15,16,17,18,19,20,20)
-W_PLAN = (2, 6, 10, 13, 14, 15)
-Y_ON_V = [(h, 3) for h in range(5)]
-CAST_ON_V = ()
-MXB = 8
-YG = 3
+LATE_UNITS = 3
+VECTOR_SLOTS = 3
+TURN_STEP = 3
+FIRST_IMAGE_TURN = 10
+LOAD_LEAD = 4
+BIG_TILES = 15
+WARM_UP = (16, 10, 8)
 
 
 def tile_contrastive_two_tower_embeddings_g1_kernel(
@@ -47,30 +46,47 @@ def tile_contrastive_two_tower_embeddings_g1_kernel(
     w_in = {"img": w_image, "txt": w_text}
     first_row = {"img": 0, "txt": NI}
 
+    def span(j):
+        return slice(j * SPAN, (j + 1) * SPAN)
+
+    def cols(j):
+        return slice(j * P, (j + 1) * P)
+
     def unit_of(r):
-        if r < TXT_ROUNDS:
+        if r < TEXT_ROUNDS:
             return ("txt", r // 4, r // 2 % 2)
-        return ("img", (r - TXT_ROUNDS) // 2, r % 2)
+        return ("img", (r - TEXT_ROUNDS) // 2, r % 2)
 
     def ended(tower, r):
         if 0 <= r < ROUNDS and unit_of(r)[0] == tower and (tower == "img" or r % 2 == 1):
             return unit_of(r)
         return None
 
-    x_jobs = [("txt", b, c, h) for b in range(1, 4) for c in range(2) for h in range(2)]
-    x_jobs += [("img", b, c, 0) for b in range(4) for c in range(3)]
-    x_plan, w_plan = {}, {}
-    for job, at in zip(x_jobs, A_PLAN):
-        x_plan.setdefault(at, []).append(job)
-    for job, at in zip([("img", c, g) for c in range(3) for g in range(2)], W_PLAN):
-        w_plan.setdefault(at, []).append(job)
+    def first_use(tower, b):
+        return 4 * b if tower == "txt" else TEXT_ROUNDS + 2 * b
 
-    def needed(job):
-        return 4 * job[1] if job[0] == "txt" else TXT_ROUNDS + 2 * job[1]
+    x_plan = {r: [] for r in range(ROUNDS)}
+    for b in range(1, BLOCKS):
+        for k in range(4):
+            r = 1 + k // 2 if b == 1 else TURN_STEP * (b - 1) + k
+            x_plan[r].append(("txt", b, k // 2, k % 2))
+    for b in range(BLOCKS):
+        for c in range(PASSES["img"]):
+            r = min(FIRST_IMAGE_TURN + TURN_STEP * b + c, first_use("img", b) - 2)
+            x_plan[r].append(("img", b, c, 0))
+
+    rounding = {}
+    for n in range(TEXT_UNITS):
+        late = n - (TEXT_UNITS - LATE_UNITS)
+        rounding[2 * n + 3 if late < 0 else TEXT_ROUNDS + 1 + late] = unit_of(2 * n)
+
+    w_jobs = [("img", c, g) for c in range(PASSES["img"]) for g in range(HALVES)]
+    early = len(w_jobs) - LATE_UNITS
+    w_plan = {4 * n + 2 if n < early else TEXT_ROUNDS - len(w_jobs) + n: job for n, job in enumerate(w_jobs)}
 
     with ExitStack() as ctx:
         keep = ctx.enter_context(tc.tile_pool(name="keep", bufs=1))
-        work = ctx.enter_context(tc.tile_pool(name="work", bufs=2))
+        work = ctx.enter_context(tc.tile_pool(name="work", bufs=1))
         psum = ctx.enter_context(tc.psum_pool(name="psum", bufs=8))
         ctx.enter_context(tc.manual_schedule())
 
@@ -81,85 +97,84 @@ def tile_contrastive_two_tower_embeddings_g1_kernel(
         for tower, rows in (("img", NI), ("txt", NT)):
             w_codes[tower] = keep.tile([P, PASSES[tower], N], U32, name="w_codes_" + tower, align_bytes=64)
             w_scales[tower] = keep.tile([P, PASSES[tower], N], U8, name="w_scales_" + tower, align_bytes=64)
-            y_scales[tower] = keep.tile([P, 2, rows], U8, name="y_scales_" + tower, align_bytes=64)
-        bt = keep.tile([P, 2, PACK], BF16, name="bt")
-        gt = keep.tile([P, 2, PACK], BF16, name="gt")
-        bi = keep.tile([P, 2, PACK], BF16, name="bi")
+            y_scales[tower] = keep.tile([P, HALVES, rows], U8, name="y_scales_" + tower, align_bytes=64)
+        bt = keep.tile([P, HALVES, PACK], BF16, name="bt")
+        gt = keep.tile([P, HALVES, PACK], BF16, name="gt")
+        bi = keep.tile([P, HALVES, PACK], BF16, name="bi")
         bi_rows = keep.tile([P, N], BF16, name="bi_rows")
 
         x_raw, x_grouped, x_codes, x_scales = {}, {}, {}, {}
         w_raw, w_grouped = {}, {}
-        v_t, y_rows, y_bf, y_grouped = {}, {}, {}, {}
+        v_t, y_rows, u_pairs, y_grouped = {}, {}, {}, {}
 
-        spare = list(range(SLOTS))
-        slot_of = {}
+        spare = list(range(BIG_TILES))
+        place = {}
 
         def take(key, shape, dtype):
-            slot_of[key] = spare[0]
+            place[key] = spare[0]
             spare.remove(spare[0])
-            return work.tile(shape, dtype, name="big", tag="slot%d" % slot_of[key], bufs=1)
+            return work.tile(shape, dtype, name="big", tag="big%d" % place[key])
 
         def give(key):
-            spare.append(slot_of[key])
+            spare.append(place[key])
 
-        def bank(kind):
-            if MXB == 8:
-                return psum.tile([P, BANK], F32, name="bank", tag="bank", bufs=8)
-            return psum.tile([P, BANK], F32, name="bank", tag=kind, bufs=MXB if kind == "mx" else 8 - MXB)
-
-        def half(g):
-            return slice(g * KP, (g + 1) * KP)
+        def bank():
+            return psum.tile([P, SPAN], F32, name="bank", tag="bank")
 
         def load_vector(tile, vector):
-            nc.sync.dma_start(out=tile[:], in_=vector.rearrange("(g p t) -> p g t", g=2, t=PACK))
+            nc.sync.dma_start(out=tile[:], in_=vector.rearrange("(g p t) -> p g t", g=HALVES, t=PACK))
 
         def load_w(tower, c, halves):
-            cols = slice(halves[0] * KP, (halves[-1] + 1) * KP)
-            raw = take(("w", tower, c, halves[-1]), [P, PACK, len(halves) * KP], BF16)
-            nc.sync.dma_start(out=raw[:], in_=w_in[tower][half(c), cols].rearrange("(p j) n -> p j n", j=PACK))
+            features = slice(halves[0] * SPAN, (halves[-1] + 1) * SPAN)
+            raw = take(("w", tower, c, halves[-1]), [P, PACK, len(halves) * SPAN], BF16)
+            nc.sync.dma_start(out=raw[:], in_=w_in[tower][span(c), features].rearrange("(p j) n -> p j n", j=PACK))
             for g in halves:
-                w_raw[tower, c, g] = raw[:, :, half(g - halves[0])]
+                w_raw[tower, c, g] = raw[:, :, span(g - halves[0])]
 
         def load_x(tower, b, pairs):
             rows = ROWS[tower]
-            src = x_in[tower][b * rows : (b + 1) * rows, :].rearrange("(p i) k -> p i k" if tower == "txt" else "(i p) k -> p i k", p=P)
+            order = "(r i) k -> r i k" if tower == "txt" else "(i r) k -> r i k"
+            src = x_in[tower][b * rows : (b + 1) * rows, :].rearrange(order, r=P)
             src = src[:, 2 * pairs[0] : 2 * pairs[-1] + 2, :]
             raw = take(("x", tower, b, pairs[-1]), list(src.shape), BF16)
             nc.sync.dma_start(out=raw[:], in_=src)
             for h in pairs:
                 x_raw[tower, b, h] = raw[:, 2 * (h - pairs[0]) : 2 * (h - pairs[0]) + 2, :].bitcast(F32)
 
-        def interleave_w(job, copy, lo, hi):
-            tower, c, g = job
-            if job not in w_grouped:
-                w_grouped[job] = work.tile([P, PACK * KP], BF16, name="w_grouped", tag="w_grouped", bufs=3, align_bytes=64)
-            raw, grouped = w_raw[job][:, :, lo:hi], w_grouped[job]
-            if tower == "img":
-                dst = grouped[:, PACK * lo : PACK * hi].rearrange("p (a i j) -> p a j i", i=4, j=PACK)
-                copy(out=dst, in_=raw.rearrange("p j (a i) -> p a j i", i=4))
-            else:
-                dst = grouped[:].rearrange("p (t a b j) -> p a t b j", t=PACK, b=2, j=PACK)[:, lo // 8 : hi // 8]
-                copy(out=dst, in_=raw.rearrange("p j (a b t) -> p a t b j", b=2, t=PACK))
+        def w_tile(job):
+            w_grouped[job] = work.tile([P, PACK * SPAN], BF16, name="w_grouped", tag="w_grouped", bufs=3, align_bytes=64)
+            return w_grouped[job]
+
+        def group_w_image(job):
+            nc.vector.tensor_copy(
+                out=w_tile(job)[:].rearrange("p (a i j) -> p a j i", i=4, j=PACK),
+                in_=w_raw[job].rearrange("p j (a i) -> p a j i", i=4),
+            )
+
+        def group_w_text(job):
+            grouped = w_tile(job)
+            src = w_raw[job].rearrange("p j (a b t) -> p a t b j", b=2, t=PACK)
+            for copy, lo, hi in ((nc.vector.tensor_copy, 0, VECTOR_SLOTS), (nc.scalar.copy, VECTOR_SLOTS, PACK)):
+                dst = grouped[:, lo * SPAN : hi * SPAN].rearrange("p (t a b j) -> p a t b j", t=hi - lo, b=2, j=PACK)
+                copy(out=dst, in_=src[:, :, lo:hi])
 
         def quantize_w(job):
             tower, c, g = job
             nc.vector.quantize_mx(
-                out=w_codes[tower][:, c, half(g)].bitcast(FP8X4),
-                scales=w_scales[tower][:, c, half(g)],
+                out=w_codes[tower][:, c, span(g)].bitcast(FP8X4),
+                scales=w_scales[tower][:, c, span(g)],
                 in_=w_grouped[job][:],
             )
 
         def turn_x(job):
             tower, b, c, h = job
-            ps = bank("turn")
+            ps = bank()
             for i in range(2):
                 for u in range(2):
-                    words = x_raw[tower, b, h][:, i, c * 256 + u : (c + 1) * 256 : 2]
-                    nc.tensor.transpose(ps[:, (2 * i + u) * P : (2 * i + u + 1) * P], words, ident[:])
+                    pairs = x_raw[tower, b, h][:, i, c * PAIRS + u : (c + 1) * PAIRS : 2]
+                    nc.tensor.transpose(ps[:, cols(2 * i + u)], pairs, ident[:])
             if h == 0:
-                x_grouped[tower, b, c] = work.tile(
-                    [P, PACK * ROWS[tower]], BF16, name="x_grouped", tag="x_grouped", bufs=4, align_bytes=64
-                )
+                x_grouped[tower, b, c] = work.tile([P, PACK * ROWS[tower]], BF16, name="x_grouped", tag="x_grouped", bufs=4, align_bytes=64)
             dst = x_grouped[tower, b, c][:].bitcast(F32)
             if tower == "img":
                 dst = dst.rearrange("p (i r u) -> p i r u", i=2, u=2)
@@ -167,27 +182,26 @@ def tile_contrastive_two_tower_embeddings_g1_kernel(
             else:
                 dst = dst.rearrange("p (r i u) -> p r i u", i=4, u=2)[:, :, 2 * h : 2 * h + 2, :]
                 src = ps[:].rearrange("p (i u r) -> p r i u", i=2, u=2)
-            return lambda: nc.scalar.copy(out=dst, in_=src)
+            nc.scalar.copy(out=dst, in_=src)
 
         def quantize_x(job):
             tower, b, c, h = job
             if tower == "txt" and h == 0:
                 return
-            bufs = 9 if tower == "img" else 4
-            codes = work.tile([P, ROWS[tower]], U32, name="x_codes", tag="x_codes_" + tower, bufs=bufs, align_bytes=64)
-            scales = work.tile([P, ROWS[tower]], U8, name="x_scales", tag="x_scales_" + tower, bufs=bufs, align_bytes=64)
+            bufs = PASSES[tower] * (3 if tower == "img" else 2)
+            codes = work.tile([P, ROWS[tower]], U32, name="x_codes_" + tower, tag="x_codes_" + tower, bufs=bufs, align_bytes=64)
+            scales = work.tile([P, ROWS[tower]], U8, name="x_scales_" + tower, tag="x_scales_" + tower, bufs=bufs, align_bytes=64)
             nc.vector.quantize_mx(out=codes[:].bitcast(FP8X4), scales=scales[:], in_=x_grouped[tower, b, c][:])
             x_codes[tower, b, c], x_scales[tower, b, c] = codes, scales
 
         def mx_pass(unit, s, c, ps):
             tower, b, g = unit
             xc, xs = x_codes[tower, b, c], x_scales[tower, b, c]
-            wc, ws = w_codes[tower][:, c, half(g)], w_scales[tower][:, c, half(g)]
-            still = slice(s * P, (s + 1) * P)
+            wc, ws = w_codes[tower][:, c, span(g)], w_scales[tower][:, c, span(g)]
             if tower == "img":
-                lhs, lhs_s, rhs, rhs_s = xc[:, still], xs[:, still], wc, ws
+                lhs, lhs_s, rhs, rhs_s = xc[:, cols(s)], xs[:, cols(s)], wc, ws
             else:
-                lhs, lhs_s, rhs, rhs_s = wc[:, still], ws[:, still], xc[:], xs[:]
+                lhs, lhs_s, rhs, rhs_s = wc[:, cols(s)], ws[:, cols(s)], xc[:], xs[:]
             nc.tensor.matmul_mx(
                 out=ps[:],
                 lhsT=lhs.bitcast(FP8X4),
@@ -199,25 +213,25 @@ def tile_contrastive_two_tower_embeddings_g1_kernel(
             )
 
         def product(unit, s):
-            ps = bank("mx")
+            ps = bank()
             for c in range(PASSES[unit[0]]):
                 mx_pass(unit, s, c, ps)
             return ps
 
-        def y_tile(key):
+        def y_tile(key, width):
             if key not in y_rows:
-                y_rows[key] = take(("y",) + key, [P, 2, N], F32)
+                y_rows[key] = take(("y",) + key, [P, 2, width], F32)
             return y_rows[key]
 
         def add_bias(unit, s, ps):
-            tower, b, g = unit
-            nc.vector.tensor_tensor(out=y_tile((tower, b))[:, s, half(g)], in0=ps[:], in1=bi_rows[:, half(g)], op=ALU.add)
+            nc.vector.tensor_tensor(out=y_tile(unit, SPAN)[:, s, :], in0=ps[:], in1=bi_rows[:, span(unit[2])], op=ALU.add)
 
-        def image_rows(b):
-            return out_0[b * ROWS["img"] : (b + 1) * ROWS["img"], :].rearrange("(i r) n -> r i n", i=2)
+        def u_out(unit):
+            tower, b, g = unit
+            return out_0[b * ROWS[tower] : (b + 1) * ROWS[tower], span(g)].rearrange("(i r) n -> r i n", i=2)
 
         def squash(unit, t, ps):
-            if unit not in v_t:
+            if t == 0:
                 v_t[unit] = take(("v", unit), [P, PACK, ROWS["txt"]], F32)
             nc.scalar.activation(out=v_t[unit][:, t, :], in_=ps[:], func=ACT.Tanh, bias=bt[:, unit[2], t : t + 1])
 
@@ -228,9 +242,7 @@ def tile_contrastive_two_tower_embeddings_g1_kernel(
                 nc.vector.tensor_scalar(out=v, in0=v, scalar1=gt[:, unit[2], t : t + 1], scalar2=None, op0=ALU.mult)
 
         def grouped_tile(unit):
-            y_grouped[unit] = work.tile(
-                [P, PACK * ROWS[unit[0]]], BF16, name="y_grouped", tag="y_grouped", bufs=YG, align_bytes=64
-            )
+            y_grouped[unit] = work.tile([P, PACK * ROWS[unit[0]]], BF16, name="y_grouped", tag="y_grouped", bufs=3, align_bytes=64)
             return y_grouped[unit]
 
         def round_v(unit):
@@ -239,20 +251,21 @@ def tile_contrastive_two_tower_embeddings_g1_kernel(
                 in_=v_t[unit][:].rearrange("p t (a i) -> p a t i", i=4),
             )
 
+        def pairs_tile(unit):
+            u_pairs[unit] = work.tile([P, 2 * SPAN], BF16, name="u_pairs", tag="u_pairs", bufs=3)
+            return u_pairs[unit]
+
         def round_u(unit):
-            tower, b, g = unit
-            y_bf[unit] = work.tile([P, 2 * KP], BF16, name="y_bf", tag="y_bf", bufs=3)
-            copy = nc.vector.tensor_copy if unit[1:] in CAST_ON_V else nc.scalar.copy
-            copy(
-                out=y_bf[unit][:].rearrange("r (i u p e) -> r i u p e", i=2, u=2, e=2),
-                in_=y_rows[tower, b][:, :, half(g)].rearrange("r i (p u e) -> r i u p e", u=2, e=2),
+            nc.scalar.copy(
+                out=pairs_tile(unit)[:].rearrange("r (i u p e) -> r i u p e", i=2, u=2, e=2),
+                in_=y_rows[unit][:].rearrange("r i (p u e) -> r i u p e", u=2, e=2),
             )
 
         def turn_u(unit):
-            ps = bank("turn")
-            words = y_bf[unit][:].bitcast(F32)
+            ps = bank()
+            pairs = u_pairs[unit][:].bitcast(F32)
             for q in range(4):
-                nc.tensor.transpose(ps[:, q * P : (q + 1) * P], words[:, q * P : (q + 1) * P], ident[:])
+                nc.tensor.transpose(ps[:, cols(q)], pairs[:, cols(q)], ident[:])
             nc.scalar.copy(
                 out=grouped_tile(unit)[:].bitcast(F32).rearrange("p (i r u) -> p i r u", i=2, u=2),
                 in_=ps[:].rearrange("p (i u r) -> p i r u", i=2, u=2),
@@ -260,14 +273,13 @@ def tile_contrastive_two_tower_embeddings_g1_kernel(
 
         def turn_v(unit, i):
             tower, b, g = unit
-            ps = bank("turn")
+            ps = bank()
             for t in range(PACK):
-                nc.tensor.transpose(ps[:, t * P : (t + 1) * P], v_t[unit][:, t, i * P : (i + 1) * P], ident[:])
-            dst = y_tile((tower, b, i // 2))[:, i % 2, half(g)]
-            copy = nc.vector.tensor_copy if (2 * b + g, i) in Y_ON_V else nc.scalar.copy
-            return lambda: copy(
-                out=dst.rearrange("r (p t) -> r p t", t=PACK), in_=ps[:].rearrange("r (t p) -> r p t", t=PACK)
-            )
+                nc.tensor.transpose(ps[:, cols(t)], v_t[unit][:, t, cols(i)], ident[:])
+            dst = y_tile((tower, b, i // 2), N)[:, i % 2, span(g)]
+            on_vector = i == 3 and HALVES * b + g < TEXT_UNITS - LATE_UNITS
+            copy = nc.vector.tensor_copy if on_vector else nc.scalar.copy
+            copy(out=dst.rearrange("r (p t) -> r p t", t=PACK), in_=ps[:].rearrange("r (t p) -> r p t", t=PACK))
 
         def store_v(b, pair):
             m0 = NI + b * ROWS["txt"] + pair * 2 * P
@@ -296,36 +308,36 @@ def tile_contrastive_two_tower_embeddings_g1_kernel(
             nc.sync.dma_start(out=words_out[g, :, m0 : m0 + rows], in_=codes[:].bitcast(I32))
 
         def spread_bias():
-            ps = bank("turn")
-            words = bi[:].rearrange("p g t -> p (g t)").bitcast(F32)
+            ps = bank()
+            pairs = bi[:].rearrange("p g t -> p (g t)").bitcast(F32)
             for q in range(4):
-                nc.tensor.transpose(ps[:, q * P : (q + 1) * P], words[:, q : q + 1].to_broadcast([P, P]), ident[:])
+                nc.tensor.transpose(ps[:, cols(q)], pairs[:, q : q + 1].to_broadcast([P, P]), ident[:])
             nc.scalar.copy(
-                out=bi_rows[:].bitcast(F32).rearrange("r (g p u) -> r g p u", g=2, u=2),
-                in_=ps[:].rearrange("r (g u p) -> r g p u", g=2, u=2),
+                out=bi_rows[:].bitcast(F32).rearrange("r (g p u) -> r g p u", g=HALVES, u=2),
+                in_=ps[:].rearrange("r (g u p) -> r g p u", g=HALVES, u=2),
             )
 
         loads = []
         for r in range(ROUNDS):
-            loads += [(r, "w", job) for job in w_plan.get(r, []) if job[2] == 0]
-            loads += [(r, "x", job) for job in x_plan.get(r, []) if job[2:] == (0, 0)]
+            if r in w_plan and w_plan[r][2] == 0:
+                loads.append((r, load_w, w_plan[r][:2] + ((0, 1),)))
+            for tower, b, c, h in x_plan[r]:
+                if c == 0 and h == 0:
+                    loads.append((r, load_x, (tower, b, (0,) if tower == "img" else (0, 1))))
 
         def issue_loads(now):
-            while loads and loads[0][0] <= now + LEAD:
-                r, kind, job = loads[0]
+            while loads and loads[0][0] <= now + LOAD_LEAD:
+                loads[0][1](*loads[0][2])
                 loads.remove(loads[0])
-                if kind == "w":
-                    load_w(job[0], job[1], (0, 1))
-                else:
-                    load_x(job[0], job[1], (0,) if job[0] == "img" else (0, 1))
 
         warm_codes = keep.tile([P, P], U32, name="warm_codes", align_bytes=64)
         warm_scales = keep.tile([P, P], U8, name="warm_scales", align_bytes=64)
+        zeros = work.tile([P, SPAN], BF16, name="zeros", tag="w_grouped", bufs=3, align_bytes=64)
+        nc.vector.memset(zeros[:], 0.0)
+        nc.vector.quantize_mx(out=warm_codes[:].bitcast(FP8X4), scales=warm_scales[:], in_=zeros[:])
 
-        def warm(n):
-            if n == 0:
-                return
-            ps = bank("turn")
+        def warm_up(n):
+            ps = bank()
             for k in range(n):
                 nc.tensor.matmul_mx(
                     out=ps[:, :P],
@@ -337,14 +349,6 @@ def tile_contrastive_two_tower_embeddings_g1_kernel(
                     stop=True,
                 )
 
-        def share_w(job):
-            interleave_w(job, nc.vector.tensor_copy, 0, HEAD_V_COLS)
-            interleave_w(job, nc.scalar.copy, HEAD_V_COLS, KP)
-
-        if sum(WARM):
-            warm_in = work.tile([P, KP], BF16, name="warm_in", tag="w_grouped", bufs=3, align_bytes=64)
-            nc.vector.memset(warm_in[:], 0.0)
-            nc.vector.quantize_mx(out=warm_codes[:].bitcast(FP8X4), scales=warm_scales[:], in_=warm_in[:])
         load_vector(bi, b_image)
         for k in range(2):
             load_x("txt", 0, (k,))
@@ -353,29 +357,29 @@ def tile_contrastive_two_tower_embeddings_g1_kernel(
             load_w("txt", c, (1,))
         load_vector(bt, b_text)
         load_vector(gt, g_text)
-        warm(WARM[0])
+        warm_up(WARM_UP[0])
         spread_bias()
         for c in range(2):
-            turn_x(("txt", 0, c, 0))()
-        share_w(("txt", 0, 0))
+            turn_x(("txt", 0, c, 0))
+        group_w_text(("txt", 0, 0))
         quantize_w(("txt", 0, 0))
-        warm(WARM[1])
+        warm_up(WARM_UP[1])
         for c in range(2):
-            turn_x(("txt", 0, c, 1))()
+            turn_x(("txt", 0, c, 1))
         issue_loads(1)
-        warm(WARM[2])
-        share_w(("txt", 1, 0))
+        warm_up(WARM_UP[2])
+        group_w_text(("txt", 1, 0))
         for c in range(2):
             quantize_x(("txt", 0, c, 1))
         quantize_w(("txt", 1, 0))
-        share_w(("txt", 0, 1))
+        group_w_text(("txt", 0, 1))
         quantize_w(("txt", 0, 1))
-        share_w(("txt", 1, 1))
+        group_w_text(("txt", 1, 1))
         for k in range(2):
             give(("x", "txt", 0, k))
             give(("w", "txt", k, 0))
             give(("w", "txt", k, 1))
-        first = [bank("mx" if t < MXB else "turn") for t in range(PACK)]
+        first = [bank() for t in range(PACK)]
         for c in range(2):
             for t in range(PACK):
                 mx_pass(unit_of(0), t, c, first[t])
@@ -384,100 +388,93 @@ def tile_contrastive_two_tower_embeddings_g1_kernel(
         quantize_w(("txt", 1, 1))
         gain(0)
         for job in x_plan[1]:
-            turn_x(job)()
+            turn_x(job)
 
         last = ROUNDS - 1
         for r in range(2, last):
             unit = unit_of(r)
-            lagged = [job for job in x_plan.get(r - 2, []) if r - 1 < TXT_ROUNDS and r < needed(job) and r > 2]
-            prompt = [job for job in x_plan.get(r - 1, []) if not (r < TXT_ROUNDS and r + 1 < needed(job))]
-            if r - 1 < TXT_ROUNDS:
+            text_round = r < TEXT_ROUNDS
+            relaxed = [job for job in x_plan[r - 2] if r - 1 < TEXT_ROUNDS and r < first_use(*job[:2])]
+            prompt = [job for job in x_plan[r - 1] if not (text_round and r + 1 < first_use(*job[:2]))]
+
+            if r - 1 < TEXT_ROUNDS:
                 gain(r - 1)
-            for job in lagged:
+            for job in relaxed:
                 quantize_x(job)
             if ended("img", r - 1):
                 round_u(ended("img", r - 1))
-                if unit[2] == 0:
-                    give(("y",) + ended("img", r - 1)[:2])
-            for job in w_plan.get(r - 1, []):
-                quantize_w(job)
-            for q in range(1, TXT_ROUNDS, 2):
-                if IL_AT.get(q, q + 2) == r - 1:
-                    quantize_y(unit_of(q))
+                give(("y",) + ended("img", r - 1))
+            if r - 1 in w_plan:
+                quantize_w(w_plan[r - 1])
+            if r - 1 in rounding:
+                quantize_y(rounding[r - 1])
             if ended("img", r - 3):
                 quantize_y(ended("img", r - 3))
-            if max(IL_AT.get(q, q + 2) for q in range(1, TXT_ROUNDS, 2)) == r - 1:
+            if r - 1 == max(rounding):
                 store_scales("txt", [nc.sync])
-            if unit[0] == "txt":
+            if text_round:
                 for job in prompt:
                     quantize_x(job)
-            for q in range(1, TXT_ROUNDS, 2):
-                if IL_AT.get(q, q + 2) == r and unit[0] == "txt":
-                    round_v(unit_of(q))
-                if max(IL_AT.get(q, q + 2), q + 3) == r - 1:
-                    give(("v", unit_of(q)))
-            for job in w_plan.get(r, []):
-                interleave_w(job, nc.vector.tensor_copy, 0, KP)
-                if job[2] == 1:
-                    give(("w", job[0], job[1], 1))
-            if unit[0] == "txt":
+                if r in rounding:
+                    round_v(rounding[r])
+            for rounded, done in rounding.items():
+                if max(rounded, 4 * done[1] + 2 * done[2] + 4) == r - 1:
+                    give(("v", done))
+            if r in w_plan:
+                group_w_image(w_plan[r])
+                if w_plan[r][2] == 1:
+                    give(("w",) + w_plan[r])
+
+            if text_round:
                 banks = [product(unit, 2 * (r % 2) + s) for s in range(2)]
-                for s in (1, 0):
+                for s in range(2):
                     squash(unit, 2 * (r % 2) + s, banks[s])
             else:
                 add_bias(unit, 0, product(unit, 0))
                 for job in prompt:
                     quantize_x(job)
                 add_bias(unit, 1, product(unit, 1))
-                for q in range(1, TXT_ROUNDS, 2):
-                    if IL_AT.get(q, q + 2) == r:
-                        round_v(unit_of(q))
-                if unit[2] == 1:
-                    nc.sync.dma_start(out=image_rows(unit[1]), in_=y_rows[unit[:2]][:])
-                elif r == last - 1:
-                    nc.sync.dma_start(out=image_rows(unit[1])[:, :, half(0)], in_=y_rows[unit[:2]][:, :, half(0)])
-            copies = []
-            for job in x_plan.get(r, []):
-                copies.append(turn_x(job))
-                if job[2:] == ((2, 0) if job[0] == "img" else (1, 1)):
+                if r in rounding:
+                    round_v(rounding[r])
+                nc.sync.dma_start(out=u_out(unit), in_=y_rows[unit][:])
+
+            for job in x_plan[r]:
+                turn_x(job)
+                if job[2:] == ((PASSES["img"] - 1, 0) if job[0] == "img" else (PASSES["txt"] - 1, 1)):
                     give(("x", job[0], job[1], job[3]))
-            for pair in range(2):
-                source = ended("txt", r - 2 - pair)
-                if source:
-                    copies += [turn_v(source, 2 * pair), turn_v(source, 2 * pair + 1)]
-            for copy in reversed(copies) if unit[0] == "txt" else copies:
-                copy()
-            for pair in range(2):
-                source = ended("txt", r - 2 - pair)
-                if source and source[2] == 1:
+            sources = [(ended("txt", r - 2 - pair), pair) for pair in range(2) if ended("txt", r - 2 - pair)]
+            for source, pair in sources:
+                turn_v(source, 2 * pair)
+                turn_v(source, 2 * pair + 1)
+            for source, pair in sources:
+                if source[2] == HALVES - 1:
                     store_v(source[1], pair)
             if ended("img", r - 2):
                 turn_u(ended("img", r - 2))
             issue_loads(r)
 
         unit = unit_of(last)
-        tower, b, g = unit
         turn_u(unit_of(last - 2))
         round_u(unit_of(last - 1))
         quantize_y(unit_of(last - 3))
-        y_bf[unit] = work.tile([P, 2 * KP], BF16, name="y_bf", tag="y_bf", bufs=3)
+        pairs_tile(unit)
         quantize_y(unit_of(last - 2))
         banks = [product(unit, s) for s in range(2)]
         for s in range(2):
             nc.vector.tensor_tensor(
-                out=y_bf[unit][:, half(s)].rearrange("r (u p e) -> r u p e", u=2, e=2),
+                out=u_pairs[unit][:, span(s)].rearrange("r (u p e) -> r u p e", u=2, e=2),
                 in0=banks[s][:].rearrange("r (p u e) -> r u p e", u=2, e=2),
-                in1=bi_rows[:, half(g)].rearrange("r (p u e) -> r u p e", u=2, e=2),
+                in1=bi_rows[:, span(unit[2])].rearrange("r (p u e) -> r u p e", u=2, e=2),
                 op=ALU.add,
             )
             add_bias(unit, s, banks[s])
-            nc.sync.dma_start(out=image_rows(b)[:, s, half(g)], in_=y_rows[tower, b][:, s, half(g)])
+            nc.sync.dma_start(out=u_out(unit)[:, s, :], in_=y_rows[unit][:, s, :])
         turn_u(unit_of(last - 1))
-        words, grouped = y_bf[unit][:].bitcast(F32), grouped_tile(unit)[:].bitcast(F32)
+        pairs, grouped = u_pairs[unit][:].bitcast(F32), grouped_tile(unit)[:].bitcast(F32)
         for s in range(2):
-            ps = bank("turn")
+            ps = bank()
             for u in range(2):
-                nc.tensor.transpose(ps[:, u * P : (u + 1) * P], words[:, (2 * s + u) * P : (2 * s + u + 1) * P], ident[:])
+                nc.tensor.transpose(ps[:, cols(u)], pairs[:, cols(2 * s + u)], ident[:])
             nc.scalar.copy(
                 out=grouped[:, 2 * s * P : 2 * (s + 1) * P].rearrange("p (r u) -> p r u", u=2),
                 in_=ps[:, : 2 * P].rearrange("p (u r) -> p r u", u=2),

@@ -18,7 +18,6 @@ ACT = mybir.ActivationFunctionType
 P = 128
 PACK = 4
 SPAN = P * PACK
-PAIRS = SPAN // 2
 HALVES = N // SPAN
 ROWS = {"img": 256, "txt": 512}
 PASSES = {"img": KI // SPAN, "txt": KT // SPAN}
@@ -27,12 +26,10 @@ TEXT_UNITS = BLOCKS * HALVES
 TEXT_ROUNDS = 2 * TEXT_UNITS
 ROUNDS = TEXT_ROUNDS + BLOCKS * HALVES
 
-LATE_UNITS = 3
-VECTOR_SLOTS = 3
-TURN_STEP = 3
-FIRST_IMAGE_TURN = 10
-LOAD_LEAD = 4
-BIG_TILES = 15
+VECTOR_COLUMNS = 320
+PRODUCT_BANKS = 3
+RAW_X_TILES = 4
+RAW_W_TILES = 5
 WARM_UP = (16, 10, 8)
 
 
@@ -52,111 +49,94 @@ def tile_contrastive_two_tower_embeddings_g1_kernel(
     def cols(j):
         return slice(j * P, (j + 1) * P)
 
+    text_units = [("txt", b, g) for g in range(HALVES) for b in range(2)]
+    text_units += [("txt", b, g) for b in range(2, BLOCKS) for g in range(HALVES)]
+    image_units = [("img", b, g) for b in range(BLOCKS) for g in range(HALVES)]
+
     def unit_of(r):
-        if r < TEXT_ROUNDS:
-            return ("txt", r // 4, r // 2 % 2)
-        return ("img", (r - TEXT_ROUNDS) // 2, r % 2)
+        return text_units[r // 2] if r < TEXT_ROUNDS else image_units[r - TEXT_ROUNDS]
 
     def ended(tower, r):
         if 0 <= r < ROUNDS and unit_of(r)[0] == tower and (tower == "img" or r % 2 == 1):
             return unit_of(r)
         return None
 
-    def first_use(tower, b):
-        return 4 * b if tower == "txt" else TEXT_ROUNDS + 2 * b
+    x_jobs = [("txt", b, c, h) for b in range(2, BLOCKS) for c in range(PASSES["txt"]) for h in range(2)]
+    x_jobs += [("img", b, c, 0) for b in range(BLOCKS) for c in range(PASSES["img"])]
+    x_plan = {r: [] for r in range(ROUNDS + 1)}
+    for n, job in enumerate(x_jobs):
+        x_plan[min(2 + n, ROUNDS - HALVES - 2)].append(job)
 
-    x_plan = {r: [] for r in range(ROUNDS)}
-    for b in range(1, BLOCKS):
-        for k in range(4):
-            r = 1 + k // 2 if b == 1 else TURN_STEP * (b - 1) + k
-            x_plan[r].append(("txt", b, k // 2, k % 2))
-    for b in range(BLOCKS):
-        for c in range(PASSES["img"]):
-            r = min(FIRST_IMAGE_TURN + TURN_STEP * b + c, first_use("img", b) - 2)
-            x_plan[r].append(("img", b, c, 0))
-
-    rounding = {}
-    for n in range(TEXT_UNITS):
-        late = n - (TEXT_UNITS - LATE_UNITS)
-        rounding[2 * n + 3 if late < 0 else TEXT_ROUNDS + 1 + late] = unit_of(2 * n)
-
-    w_jobs = [("img", c, g) for c in range(PASSES["img"]) for g in range(HALVES)]
-    early = len(w_jobs) - LATE_UNITS
-    w_plan = {4 * n + 2 if n < early else TEXT_ROUNDS - len(w_jobs) + n: job for n, job in enumerate(w_jobs)}
+    w_plan = {1 + c: ("txt", c, 1) for c in range(PASSES["txt"])}
+    for n in range(HALVES * PASSES["img"]):
+        w_plan[4 + 2 * n] = ("img", n % PASSES["img"], n // PASSES["img"])
 
     with ExitStack() as ctx:
         keep = ctx.enter_context(tc.tile_pool(name="keep", bufs=1))
-        work = ctx.enter_context(tc.tile_pool(name="work", bufs=1))
+        work = ctx.enter_context(tc.tile_pool(name="work", bufs=2))
         psum = ctx.enter_context(tc.psum_pool(name="psum", bufs=8))
         ctx.enter_context(tc.manual_schedule())
 
         ident = keep.tile([P, P], F32, name="ident")
         make_identity(nc, ident[:])
 
-        w_codes, w_scales, y_scales = {}, {}, {}
-        for tower, rows in (("img", NI), ("txt", NT)):
-            w_codes[tower] = keep.tile([P, PASSES[tower], N], U32, name="w_codes_" + tower, align_bytes=64)
-            w_scales[tower] = keep.tile([P, PASSES[tower], N], U8, name="w_scales_" + tower, align_bytes=64)
-            y_scales[tower] = keep.tile([P, HALVES, rows], U8, name="y_scales_" + tower, align_bytes=64)
+        w_codes = {
+            tower: keep.tile([P, PASSES[tower], N], U32, name="w_codes_" + tower, align_bytes=64) for tower in PASSES
+        }
+        w_scales = {
+            tower: keep.tile([P, PASSES[tower], N], U8, name="w_scales_" + tower, align_bytes=64) for tower in PASSES
+        }
+        y_scales = {
+            tower: keep.tile([P, HALVES, BLOCKS * ROWS[tower]], U8, name="y_scales_" + tower, align_bytes=64)
+            for tower in ROWS
+        }
         bt = keep.tile([P, HALVES, PACK], BF16, name="bt")
         gt = keep.tile([P, HALVES, PACK], BF16, name="gt")
         bi = keep.tile([P, HALVES, PACK], BF16, name="bi")
         bi_rows = keep.tile([P, N], BF16, name="bi_rows")
 
-        x_raw, x_grouped, x_codes, x_scales = {}, {}, {}, {}
+        x_raw, x_sorted, x_grouped, x_codes, x_scales = {}, {}, {}, {}, {}
         w_raw, w_grouped = {}, {}
         v_t, y_rows, u_pairs, y_grouped = {}, {}, {}, {}
 
-        spare = list(range(BIG_TILES))
-        place = {}
+        def product_bank():
+            return psum.tile([P, SPAN], F32, name="bank", tag="product", bufs=PRODUCT_BANKS)
 
-        def take(key, shape, dtype):
-            place[key] = spare[0]
-            spare.remove(spare[0])
-            return work.tile(shape, dtype, name="big", tag="big%d" % place[key])
-
-        def give(key):
-            spare.append(place[key])
-
-        def bank():
-            return psum.tile([P, SPAN], F32, name="bank", tag="bank")
+        def turn_bank():
+            return psum.tile([P, SPAN], F32, name="bank", tag="turn", bufs=8 - PRODUCT_BANKS)
 
         def load_vector(tile, vector):
             nc.sync.dma_start(out=tile[:], in_=vector.rearrange("(g p t) -> p g t", g=HALVES, t=PACK))
 
-        def load_w(tower, c, halves):
-            features = slice(halves[0] * SPAN, (halves[-1] + 1) * SPAN)
-            raw = take(("w", tower, c, halves[-1]), [P, PACK, len(halves) * SPAN], BF16)
-            nc.sync.dma_start(out=raw[:], in_=w_in[tower][span(c), features].rearrange("(p j) n -> p j n", j=PACK))
-            for g in halves:
-                w_raw[tower, c, g] = raw[:, :, span(g - halves[0])]
+        def load_w(job):
+            tower, c, g = job
+            w_raw[job] = work.tile([P, PACK, SPAN], BF16, name="w_raw", tag="w_raw", bufs=RAW_W_TILES)
+            nc.sync.dma_start(out=w_raw[job][:], in_=w_in[tower][span(c), span(g)].rearrange("(p j) n -> p j n", j=PACK))
 
-        def load_x(tower, b, pairs):
+        def load_x(tower, b, c0, c1):
             rows = ROWS[tower]
-            order = "(r i) k -> r i k" if tower == "txt" else "(i r) k -> r i k"
-            src = x_in[tower][b * rows : (b + 1) * rows, :].rearrange(order, r=P)
-            src = src[:, 2 * pairs[0] : 2 * pairs[-1] + 2, :]
-            raw = take(("x", tower, b, pairs[-1]), list(src.shape), BF16)
-            nc.sync.dma_start(out=raw[:], in_=src)
-            for h in pairs:
-                x_raw[tower, b, h] = raw[:, 2 * (h - pairs[0]) : 2 * (h - pairs[0]) + 2, :].bitcast(F32)
+            raw = work.tile([P, rows // P, (c1 - c0) * SPAN], BF16, name="x_raw", tag="x_raw", bufs=RAW_X_TILES)
+            src = x_in[tower][b * rows : (b + 1) * rows, c0 * SPAN : c1 * SPAN]
+            nc.sync.dma_start(out=raw[:], in_=src.rearrange("(i r) k -> r i k", r=P))
+            for c in range(c0, c1):
+                x_raw[tower, b, c] = raw[:, :, span(c - c0)].bitcast(F32)
 
-        def w_tile(job):
-            w_grouped[job] = work.tile([P, PACK * SPAN], BF16, name="w_grouped", tag="w_grouped", bufs=3, align_bytes=64)
-            return w_grouped[job]
+        def group_w(job, copy, lo, hi):
+            if lo == 0:
+                w_grouped[job] = work.tile(
+                    [P, PACK * SPAN], BF16, name="w_grouped", tag="w_grouped", bufs=3, align_bytes=64
+                )
+            raw, grouped = w_raw[job][:, :, lo:hi], w_grouped[job]
+            if job[0] == "img":
+                dst = grouped[:, PACK * lo : PACK * hi].rearrange("p (a i j) -> p a j i", i=4, j=PACK)
+                copy(out=dst, in_=raw.rearrange("p j (a i) -> p a j i", i=4))
+            else:
+                dst = grouped[:].rearrange("p (t m j) -> p m j t", t=PACK, j=PACK)[:, lo // PACK : hi // PACK]
+                copy(out=dst, in_=raw.rearrange("p j (m t) -> p m j t", t=PACK))
 
-        def group_w_image(job):
-            nc.vector.tensor_copy(
-                out=w_tile(job)[:].rearrange("p (a i j) -> p a j i", i=4, j=PACK),
-                in_=w_raw[job].rearrange("p j (a i) -> p a j i", i=4),
-            )
-
-        def group_w_text(job):
-            grouped = w_tile(job)
-            src = w_raw[job].rearrange("p j (a b t) -> p a t b j", b=2, t=PACK)
-            for copy, lo, hi in ((nc.vector.tensor_copy, 0, VECTOR_SLOTS), (nc.scalar.copy, VECTOR_SLOTS, PACK)):
-                dst = grouped[:, lo * SPAN : hi * SPAN].rearrange("p (t a b j) -> p a t b j", t=hi - lo, b=2, j=PACK)
-                copy(out=dst, in_=src[:, :, lo:hi])
+        def group_w_shared(job):
+            group_w(job, nc.vector.tensor_copy, 0, VECTOR_COLUMNS)
+            group_w(job, nc.scalar.copy, VECTOR_COLUMNS, SPAN)
 
         def quantize_w(job):
             tower, c, g = job
@@ -166,31 +146,35 @@ def tile_contrastive_two_tower_embeddings_g1_kernel(
                 in_=w_grouped[job][:],
             )
 
-        def turn_x(job):
+        def sort_x(job):
             tower, b, c, h = job
-            ps = bank()
+            x_sorted[job] = work.tile([P, 2, 2, P], F32, name="x_sorted", tag="x_sorted", bufs=3)
+            src = x_raw[tower, b, c][:, 2 * h : 2 * h + 2, :]
+            nc.vector.tensor_copy(out=x_sorted[job][:], in_=src.rearrange("r i (p u) -> r i u p", u=2))
+
+        def turn_x(job, copy=nc.scalar.copy):
+            tower, b, c, h = job
+            ps = turn_bank()
             for i in range(2):
                 for u in range(2):
-                    pairs = x_raw[tower, b, h][:, i, c * PAIRS + u : (c + 1) * PAIRS : 2]
+                    pairs = x_sorted[job][:, i, u, :] if job in x_sorted else x_raw[tower, b, c][:, 2 * h + i, u::2]
                     nc.tensor.transpose(ps[:, cols(2 * i + u)], pairs, ident[:])
             if h == 0:
-                x_grouped[tower, b, c] = work.tile([P, PACK * ROWS[tower]], BF16, name="x_grouped", tag="x_grouped", bufs=4, align_bytes=64)
-            dst = x_grouped[tower, b, c][:].bitcast(F32)
-            if tower == "img":
-                dst = dst.rearrange("p (i r u) -> p i r u", i=2, u=2)
-                src = ps[:].rearrange("p (i u r) -> p i r u", i=2, u=2)
-            else:
-                dst = dst.rearrange("p (r i u) -> p r i u", i=4, u=2)[:, :, 2 * h : 2 * h + 2, :]
-                src = ps[:].rearrange("p (i u r) -> p r i u", i=2, u=2)
-            nc.scalar.copy(out=dst, in_=src)
+                x_grouped[tower, b, c] = work.tile(
+                    [P, PACK * ROWS[tower]], BF16, name="x_grouped", tag="x_grouped", bufs=4, align_bytes=64
+                )
+            copy(
+                out=x_grouped[tower, b, c][:].bitcast(F32)[:, span(h)].rearrange("p (i r u) -> p i r u", i=2, u=2),
+                in_=ps[:].rearrange("p (i u r) -> p i r u", i=2, u=2),
+            )
 
         def quantize_x(job):
             tower, b, c, h = job
             if tower == "txt" and h == 0:
                 return
-            bufs = PASSES[tower] * (3 if tower == "img" else 2)
-            codes = work.tile([P, ROWS[tower]], U32, name="x_codes_" + tower, tag="x_codes_" + tower, bufs=bufs, align_bytes=64)
-            scales = work.tile([P, ROWS[tower]], U8, name="x_scales_" + tower, tag="x_scales_" + tower, bufs=bufs, align_bytes=64)
+            shape, bufs = [P, ROWS[tower]], 3 * PASSES[tower]
+            codes = work.tile(shape, U32, name="x_codes", tag="x_codes_" + tower, bufs=bufs, align_bytes=64)
+            scales = work.tile(shape, U8, name="x_scales", tag="x_scales_" + tower, bufs=bufs, align_bytes=64)
             nc.vector.quantize_mx(out=codes[:].bitcast(FP8X4), scales=scales[:], in_=x_grouped[tower, b, c][:])
             x_codes[tower, b, c], x_scales[tower, b, c] = codes, scales
 
@@ -213,26 +197,27 @@ def tile_contrastive_two_tower_embeddings_g1_kernel(
             )
 
         def product(unit, s):
-            ps = bank()
+            ps = product_bank()
             for c in range(PASSES[unit[0]]):
                 mx_pass(unit, s, c, ps)
             return ps
 
-        def y_tile(key, width):
-            if key not in y_rows:
-                y_rows[key] = take(("y",) + key, [P, 2, width], F32)
-            return y_rows[key]
+        def rows_tile(unit):
+            y_rows[unit] = work.tile([P, ROWS[unit[0]] // P, SPAN], F32, name="y_rows", tag="y_rows", bufs=4)
+
+        def rows_out(unit):
+            tower, b, g = unit
+            m0 = first_row[tower] + b * ROWS[tower]
+            return out_0[m0 : m0 + ROWS[tower], span(g)].rearrange("(i r) n -> r i n", r=P)
 
         def add_bias(unit, s, ps):
-            nc.vector.tensor_tensor(out=y_tile(unit, SPAN)[:, s, :], in0=ps[:], in1=bi_rows[:, span(unit[2])], op=ALU.add)
-
-        def u_out(unit):
-            tower, b, g = unit
-            return out_0[b * ROWS[tower] : (b + 1) * ROWS[tower], span(g)].rearrange("(i r) n -> r i n", i=2)
+            if s == 0:
+                rows_tile(unit)
+            nc.vector.tensor_tensor(out=y_rows[unit][:, s, :], in0=ps[:], in1=bi_rows[:, span(unit[2])], op=ALU.add)
 
         def squash(unit, t, ps):
             if t == 0:
-                v_t[unit] = take(("v", unit), [P, PACK, ROWS["txt"]], F32)
+                v_t[unit] = work.tile([P, PACK, ROWS["txt"]], F32, name="v_t", tag="v_t", bufs=4)
             nc.scalar.activation(out=v_t[unit][:, t, :], in_=ps[:], func=ACT.Tanh, bias=bt[:, unit[2], t : t + 1])
 
         def gain(r):
@@ -242,7 +227,9 @@ def tile_contrastive_two_tower_embeddings_g1_kernel(
                 nc.vector.tensor_scalar(out=v, in0=v, scalar1=gt[:, unit[2], t : t + 1], scalar2=None, op0=ALU.mult)
 
         def grouped_tile(unit):
-            y_grouped[unit] = work.tile([P, PACK * ROWS[unit[0]]], BF16, name="y_grouped", tag="y_grouped", bufs=3, align_bytes=64)
+            y_grouped[unit] = work.tile(
+                [P, PACK * ROWS[unit[0]]], BF16, name="y_grouped", tag="y_grouped", bufs=3, align_bytes=64
+            )
             return y_grouped[unit]
 
         def round_v(unit):
@@ -257,12 +244,12 @@ def tile_contrastive_two_tower_embeddings_g1_kernel(
 
         def round_u(unit):
             nc.scalar.copy(
-                out=pairs_tile(unit)[:].rearrange("r (i u p e) -> r i u p e", i=2, u=2, e=2),
-                in_=y_rows[unit][:].rearrange("r i (p u e) -> r i u p e", u=2, e=2),
+                out=pairs_tile(unit)[:].rearrange("r (i u p e) -> r i p u e", i=2, u=2, e=2),
+                in_=y_rows[unit][:].rearrange("r i (p u e) -> r i p u e", u=2, e=2),
             )
 
         def turn_u(unit):
-            ps = bank()
+            ps = turn_bank()
             pairs = u_pairs[unit][:].bitcast(F32)
             for q in range(4):
                 nc.tensor.transpose(ps[:, cols(q)], pairs[:, cols(q)], ident[:])
@@ -272,20 +259,15 @@ def tile_contrastive_two_tower_embeddings_g1_kernel(
             )
 
         def turn_v(unit, i):
-            tower, b, g = unit
-            ps = bank()
+            ps = turn_bank()
             for t in range(PACK):
                 nc.tensor.transpose(ps[:, cols(t)], v_t[unit][:, t, cols(i)], ident[:])
-            dst = y_tile((tower, b, i // 2), N)[:, i % 2, span(g)]
-            on_vector = i == 3 and HALVES * b + g < TEXT_UNITS - LATE_UNITS
-            copy = nc.vector.tensor_copy if on_vector else nc.scalar.copy
-            copy(out=dst.rearrange("r (p t) -> r p t", t=PACK), in_=ps[:].rearrange("r (t p) -> r p t", t=PACK))
-
-        def store_v(b, pair):
-            m0 = NI + b * ROWS["txt"] + pair * 2 * P
-            dst = out_0[m0 : m0 + 2 * P, :].rearrange("(i r) n -> r i n", i=2)
-            nc.sync.dma_start(out=dst, in_=y_rows["txt", b, pair][:])
-            give(("y", "txt", b, pair))
+            if i == 0:
+                rows_tile(unit)
+            nc.scalar.copy(
+                out=y_rows[unit][:, i, :].rearrange("r (p t) -> r p t", t=PACK),
+                in_=ps[:].rearrange("r (t p) -> r p t", t=PACK),
+            )
 
         def store_scales(tower, queues):
             lo, rows = first_row[tower], y_scales[tower].shape[2]
@@ -308,7 +290,7 @@ def tile_contrastive_two_tower_embeddings_g1_kernel(
             nc.sync.dma_start(out=words_out[g, :, m0 : m0 + rows], in_=codes[:].bitcast(I32))
 
         def spread_bias():
-            ps = bank()
+            ps = turn_bank()
             pairs = bi[:].rearrange("p g t -> p (g t)").bitcast(F32)
             for q in range(4):
                 nc.tensor.transpose(ps[:, cols(q)], pairs[:, q : q + 1].to_broadcast([P, P]), ident[:])
@@ -319,25 +301,28 @@ def tile_contrastive_two_tower_embeddings_g1_kernel(
 
         loads = []
         for r in range(ROUNDS):
-            if r in w_plan and w_plan[r][2] == 0:
-                loads.append((r, load_w, w_plan[r][:2] + ((0, 1),)))
-            for tower, b, c, h in x_plan[r]:
-                if c == 0 and h == 0:
-                    loads.append((r, load_x, (tower, b, (0,) if tower == "img" else (0, 1))))
+            loads += [("w", w_plan[r])] if r in w_plan else []
+            loads += [("x", job) for job in x_plan[r] if job[2:] == (0, 0)]
+        free = {"x": RAW_X_TILES - 4, "w": RAW_W_TILES - 2}
 
-        def issue_loads(now):
-            while loads and loads[0][0] <= now + LOAD_LEAD:
-                loads[0][1](*loads[0][2])
+        def issue_loads():
+            while loads and free[loads[0][0]] > 0:
+                kind, job = loads[0]
                 loads.remove(loads[0])
+                free[kind] -= 1
+                if kind == "w":
+                    load_w(job)
+                else:
+                    load_x(job[0], job[1], 0, PASSES[job[0]])
 
+        zeros = work.tile([P, SPAN], BF16, name="zeros", tag="w_grouped", bufs=3, align_bytes=64)
         warm_codes = keep.tile([P, P], U32, name="warm_codes", align_bytes=64)
         warm_scales = keep.tile([P, P], U8, name="warm_scales", align_bytes=64)
-        zeros = work.tile([P, SPAN], BF16, name="zeros", tag="w_grouped", bufs=3, align_bytes=64)
         nc.vector.memset(zeros[:], 0.0)
         nc.vector.quantize_mx(out=warm_codes[:].bitcast(FP8X4), scales=warm_scales[:], in_=zeros[:])
 
         def warm_up(n):
-            ps = bank()
+            ps = turn_bank()
             for k in range(n):
                 nc.tensor.matmul_mx(
                     out=ps[:, :P],
@@ -350,131 +335,122 @@ def tile_contrastive_two_tower_embeddings_g1_kernel(
                 )
 
         load_vector(bi, b_image)
-        for k in range(2):
-            load_x("txt", 0, (k,))
-            load_w("txt", k, (0,))
-        for c in range(2):
-            load_w("txt", c, (1,))
+        load_x("txt", 0, 0, 1)
+        load_w(("txt", 0, 0))
+        load_x("txt", 0, 1, 2)
+        load_x("txt", 1, 0, 1)
+        load_w(("txt", 1, 0))
+        load_x("txt", 1, 1, 2)
         load_vector(bt, b_text)
         load_vector(gt, g_text)
+        issue_loads()
         warm_up(WARM_UP[0])
         spread_bias()
-        for c in range(2):
-            turn_x(("txt", 0, c, 0))
-        group_w_text(("txt", 0, 0))
+        turn_x(("txt", 0, 0, 0))
+        turn_x(("txt", 0, 0, 1), nc.vector.tensor_copy)
+        group_w_shared(("txt", 0, 0))
+        quantize_x(("txt", 0, 0, 1))
         quantize_w(("txt", 0, 0))
         warm_up(WARM_UP[1])
-        for c in range(2):
-            turn_x(("txt", 0, c, 1))
-        issue_loads(1)
+        turn_x(("txt", 0, 1, 0))
+        turn_x(("txt", 0, 1, 1))
         warm_up(WARM_UP[2])
-        group_w_text(("txt", 1, 0))
-        for c in range(2):
-            quantize_x(("txt", 0, c, 1))
+        first = [product_bank() if t < PRODUCT_BANKS else turn_bank() for t in range(PACK)]
+        for t in range(PACK):
+            mx_pass(unit_of(0), t, 0, first[t])
+        quantize_x(("txt", 0, 1, 1))
+        group_w_shared(("txt", 1, 0))
+        turn_x(("txt", 1, 0, 0))
         quantize_w(("txt", 1, 0))
-        group_w_text(("txt", 0, 1))
-        quantize_w(("txt", 0, 1))
-        group_w_text(("txt", 1, 1))
-        for k in range(2):
-            give(("x", "txt", 0, k))
-            give(("w", "txt", k, 0))
-            give(("w", "txt", k, 1))
-        first = [bank() for t in range(PACK)]
-        for c in range(2):
-            for t in range(PACK):
-                mx_pass(unit_of(0), t, c, first[t])
+        turn_x(("txt", 1, 0, 1))
+        group_w(w_plan[1], nc.vector.tensor_copy, 0, SPAN)
+        turn_x(("txt", 1, 1, 0))
+        quantize_x(("txt", 1, 0, 1))
+        turn_x(("txt", 1, 1, 1))
+        free["x"] += 4
+        free["w"] += 3
+        issue_loads()
+        for t in range(PACK):
+            mx_pass(unit_of(0), t, 1, first[t])
         for t in range(PACK):
             squash(unit_of(0), t, first[t])
-        quantize_w(("txt", 1, 1))
+        quantize_x(("txt", 1, 1, 1))
         gain(0)
-        for job in x_plan[1]:
-            turn_x(job)
+        quantize_w(w_plan[1])
 
         last = ROUNDS - 1
         for r in range(2, last):
             unit = unit_of(r)
-            text_round = r < TEXT_ROUNDS
-            relaxed = [job for job in x_plan[r - 2] if r - 1 < TEXT_ROUNDS and r < first_use(*job[:2])]
-            prompt = [job for job in x_plan[r - 1] if not (text_round and r + 1 < first_use(*job[:2]))]
 
             if r - 1 < TEXT_ROUNDS:
                 gain(r - 1)
-            for job in relaxed:
-                quantize_x(job)
             if ended("img", r - 1):
                 round_u(ended("img", r - 1))
-                give(("y",) + ended("img", r - 1))
-            if r - 1 in w_plan:
+            if r > 2 and r - 1 in w_plan:
                 quantize_w(w_plan[r - 1])
-            if r - 1 in rounding:
-                quantize_y(rounding[r - 1])
+            if ended("txt", r - 3):
+                quantize_y(ended("txt", r - 3))
+            if r - 3 == TEXT_ROUNDS - 1:
+                store_scales("txt", [nc.sync])
             if ended("img", r - 3):
                 quantize_y(ended("img", r - 3))
-            if r - 1 == max(rounding):
-                store_scales("txt", [nc.sync])
-            if text_round:
-                for job in prompt:
-                    quantize_x(job)
-                if r in rounding:
-                    round_v(rounding[r])
-            for rounded, done in rounding.items():
-                if max(rounded, 4 * done[1] + 2 * done[2] + 4) == r - 1:
-                    give(("v", done))
+            if ended("txt", r - 2):
+                round_v(ended("txt", r - 2))
             if r in w_plan:
-                group_w_image(w_plan[r])
-                if w_plan[r][2] == 1:
-                    give(("w",) + w_plan[r])
+                group_w(w_plan[r], nc.vector.tensor_copy, 0, SPAN)
 
-            if text_round:
-                banks = [product(unit, 2 * (r % 2) + s) for s in range(2)]
-                for s in range(2):
-                    squash(unit, 2 * (r % 2) + s, banks[s])
+            if r < TEXT_ROUNDS:
+                for t in (2 * (r % 2), 2 * (r % 2) + 1):
+                    squash(unit, t, product(unit, t))
+                for job in x_plan[r - 1]:
+                    quantize_x(job)
             else:
                 add_bias(unit, 0, product(unit, 0))
-                for job in prompt:
+                for job in x_plan[r - 1]:
                     quantize_x(job)
                 add_bias(unit, 1, product(unit, 1))
-                if r in rounding:
-                    round_v(rounding[r])
-                nc.sync.dma_start(out=u_out(unit), in_=y_rows[unit][:])
+                nc.sync.dma_start(out=rows_out(unit), in_=y_rows[unit][:])
+                for job in x_plan[r + 1]:
+                    sort_x(job)
 
             for job in x_plan[r]:
                 turn_x(job)
                 if job[2:] == ((PASSES["img"] - 1, 0) if job[0] == "img" else (PASSES["txt"] - 1, 1)):
-                    give(("x", job[0], job[1], job[3]))
-            sources = [(ended("txt", r - 2 - pair), pair) for pair in range(2) if ended("txt", r - 2 - pair)]
-            for source, pair in sources:
-                turn_v(source, 2 * pair)
-                turn_v(source, 2 * pair + 1)
-            for source, pair in sources:
-                if source[2] == HALVES - 1:
-                    store_v(source[1], pair)
+                    free["x"] += 1
             if ended("img", r - 2):
                 turn_u(ended("img", r - 2))
-            issue_loads(r)
+            for pair in range(2):
+                source = ended("txt", r - 2 - pair)
+                if source:
+                    turn_v(source, 2 * pair)
+                    turn_v(source, 2 * pair + 1)
+                if source and pair == 1:
+                    nc.sync.dma_start(out=rows_out(source), in_=y_rows[source][:])
+            if r in w_plan:
+                free["w"] += 1
+            issue_loads()
 
         unit = unit_of(last)
         turn_u(unit_of(last - 2))
         round_u(unit_of(last - 1))
         quantize_y(unit_of(last - 3))
-        pairs_tile(unit)
+        pairs, grouped = pairs_tile(unit)[:], grouped_tile(unit)[:].bitcast(F32)
         quantize_y(unit_of(last - 2))
-        banks = [product(unit, s) for s in range(2)]
         for s in range(2):
+            ps = product(unit, s)
             nc.vector.tensor_tensor(
-                out=u_pairs[unit][:, span(s)].rearrange("r (u p e) -> r u p e", u=2, e=2),
-                in0=banks[s][:].rearrange("r (p u e) -> r u p e", u=2, e=2),
+                out=pairs[:, span(s)].rearrange("r (u p e) -> r u p e", u=2, e=2),
+                in0=ps[:].rearrange("r (p u e) -> r u p e", u=2, e=2),
                 in1=bi_rows[:, span(unit[2])].rearrange("r (p u e) -> r u p e", u=2, e=2),
                 op=ALU.add,
             )
-            add_bias(unit, s, banks[s])
-            nc.sync.dma_start(out=u_out(unit)[:, s, :], in_=y_rows[unit][:, s, :])
+            add_bias(unit, s, ps)
+            nc.sync.dma_start(out=rows_out(unit)[:, s, :], in_=y_rows[unit][:, s, :])
         turn_u(unit_of(last - 1))
-        pairs, grouped = u_pairs[unit][:].bitcast(F32), grouped_tile(unit)[:].bitcast(F32)
         for s in range(2):
-            ps = bank()
+            ps = turn_bank()
             for u in range(2):
-                nc.tensor.transpose(ps[:, cols(u)], pairs[:, cols(2 * s + u)], ident[:])
+                nc.tensor.transpose(ps[:, cols(u)], pairs.bitcast(F32)[:, cols(2 * s + u)], ident[:])
             nc.scalar.copy(
                 out=grouped[:, 2 * s * P : 2 * (s + 1) * P].rearrange("p (r u) -> p r u", u=2),
                 in_=ps[:, : 2 * P].rearrange("p (u r) -> p r u", u=2),

from contextlib import ExitStack

import concourse.mybir as mybir
from concourse.masks import make_identity

NI, NT, KI, KT, N = 1024, 2048, 1536, 1024, 1024
FLOPS = 2 * (NI * KI + NT * KT) * N

F32 = mybir.dt.float32
BF16 = mybir.dt.bfloat16
I32 = mybir.dt.int32
U32 = mybir.dt.uint32
U8 = mybir.dt.uint8
FP8X4 = mybir.dt.float8_e4m3fn_x4
ALU = mybir.AluOpType
ACT = mybir.ActivationFunctionType

P = 128
PACK = 4
SPAN = P * PACK
HALVES = N // SPAN
ROWS = {"img": 256, "txt": 512}
PASSES = {"img": KI // SPAN, "txt": KT // SPAN}
BLOCKS = 4
TEXT_UNITS = BLOCKS * HALVES
TEXT_ROUNDS = 2 * TEXT_UNITS
ROUNDS = TEXT_ROUNDS + BLOCKS * HALVES

VECTOR_COLUMNS = 320
PRODUCT_BANKS = 3
RAW_X_TILES = 4
RAW_W_TILES = 5
WARM_UP = (16, 10, 8)


def tile_contrastive_two_tower_embeddings_g1_kernel(
    tc, image, w_image, b_image, text, w_text, b_text, g_text, out_0, out_1, out_2
):
    nc = tc.nc
    words_out = out_1.rearrange("g p m t -> g p (m t)").bitcast(I32)
    scales_out = out_2.bitcast(I32)
    x_in = {"img": image, "txt": text}
    w_in = {"img": w_image, "txt": w_text}
    first_row = {"img": 0, "txt": NI}

    def span(j):
        return slice(j * SPAN, (j + 1) * SPAN)

    def cols(j):
        return slice(j * P, (j + 1) * P)

    text_units = [("txt", b, g) for g in range(HALVES) for b in range(2)]
    text_units += [("txt", b, g) for b in range(2, BLOCKS) for g in range(HALVES)]
    image_units = [("img", b, g) for b in range(BLOCKS) for g in range(HALVES)]

    def unit_of(r):
        return text_units[r // 2] if r < TEXT_ROUNDS else image_units[r - TEXT_ROUNDS]

    def ended(tower, r):
        if 0 <= r < ROUNDS and unit_of(r)[0] == tower and (tower == "img" or r % 2 == 1):
            return unit_of(r)
        return None

    x_jobs = [("txt", b, c, h) for b in range(2, BLOCKS) for c in range(PASSES["txt"]) for h in range(2)]
    x_jobs += [("img", b, c, 0) for b in range(BLOCKS) for c in range(PASSES["img"])]
    x_plan = {r: [] for r in range(ROUNDS + 1)}
    for n, job in enumerate(x_jobs):
        x_plan[min(2 + n, ROUNDS - HALVES - 2)].append(job)

    w_plan = {1 + c: ("txt", c, 1) for c in range(PASSES["txt"])}
    for n in range(HALVES * PASSES["img"]):
        w_plan[4 + 2 * n] = ("img", n % PASSES["img"], n // PASSES["img"])

    with ExitStack() as ctx:
        keep = ctx.enter_context(tc.tile_pool(name="keep", bufs=1))
        work = ctx.enter_context(tc.tile_pool(name="work", bufs=2))
        psum = ctx.enter_context(tc.psum_pool(name="psum", bufs=8))
        ctx.enter_context(tc.manual_schedule())

        ident = keep.tile([P, P], F32, name="ident")
        make_identity(nc, ident[:])

        w_codes = {
            tower: keep.tile([P, PASSES[tower], N], U32, name="w_codes_" + tower, align_bytes=64) for tower in PASSES
        }
        w_scales = {
            tower: keep.tile([P, PASSES[tower], N], U8, name="w_scales_" + tower, align_bytes=64) for tower in PASSES
        }
        y_scales = {
            tower: keep.tile([P, HALVES, BLOCKS * ROWS[tower]], U8, name="y_scales_" + tower, align_bytes=64)
            for tower in ROWS
        }
        bt = keep.tile([P, HALVES, PACK], BF16, name="bt")
        gt = keep.tile([P, HALVES, PACK], BF16, name="gt")
        bi = keep.tile([P, HALVES, PACK], BF16, name="bi")
        bi_rows = keep.tile([P, N], BF16, name="bi_rows")

        x_raw, x_sorted, x_grouped, x_codes, x_scales = {}, {}, {}, {}, {}
        w_raw, w_grouped = {}, {}
        v_t, y_rows, u_pairs, y_grouped = {}, {}, {}, {}

        def product_bank():
            return psum.tile([P, SPAN], F32, name="bank", tag="product", bufs=PRODUCT_BANKS)

        def turn_bank():
            return psum.tile([P, SPAN], F32, name="bank", tag="turn", bufs=8 - PRODUCT_BANKS)

        def load_vector(tile, vector):
            nc.sync.dma_start(out=tile[:], in_=vector.rearrange("(g p t) -> p g t", g=HALVES, t=PACK))

        def load_w(job):
            tower, c, g = job
            w_raw[job] = work.tile([P, PACK, SPAN], BF16, name="w_raw", tag="w_raw", bufs=RAW_W_TILES)
            nc.sync.dma_start(out=w_raw[job][:], in_=w_in[tower][span(c), span(g)].rearrange("(p j) n -> p j n", j=PACK))

        def load_x(tower, b, c0, c1):
            rows = ROWS[tower]
            raw = work.tile([P, rows // P, (c1 - c0) * SPAN], BF16, name="x_raw", tag="x_raw", bufs=RAW_X_TILES)
            src = x_in[tower][b * rows : (b + 1) * rows, c0 * SPAN : c1 * SPAN]
            nc.sync.dma_start(out=raw[:], in_=src.rearrange("(i r) k -> r i k", r=P))
            for c in range(c0, c1):
                x_raw[tower, b, c] = raw[:, :, span(c - c0)].bitcast(F32)

        def group_w(job, copy, lo, hi):
            if lo == 0:
                w_grouped[job] = work.tile(
                    [P, PACK * SPAN], BF16, name="w_grouped", tag="w_grouped", bufs=3, align_bytes=64
                )
            raw, grouped = w_raw[job][:, :, lo:hi], w_grouped[job]
            if job[0] == "img":
                dst = grouped[:, PACK * lo : PACK * hi].rearrange("p (a i j) -> p a j i", i=4, j=PACK)
                copy(out=dst, in_=raw.rearrange("p j (a i) -> p a j i", i=4))
            else:
                dst = grouped[:].rearrange("p (t m j) -> p m j t", t=PACK, j=PACK)[:, lo // PACK : hi // PACK]
                copy(out=dst, in_=raw.rearrange("p j (m t) -> p m j t", t=PACK))

        def group_w_shared(job):
            group_w(job, nc.vector.tensor_copy, 0, VECTOR_COLUMNS)
            group_w(job, nc.scalar.copy, VECTOR_COLUMNS, SPAN)

        def quantize_w(job):
            tower, c, g = job
            nc.vector.quantize_mx(
                out=w_codes[tower][:, c, span(g)].bitcast(FP8X4),
                scales=w_scales[tower][:, c, span(g)],
                in_=w_grouped[job][:],
            )

        def sort_x(job):
            tower, b, c, h = job
            x_sorted[job] = work.tile([P, 2, 2, P], F32, name="x_sorted", tag="x_sorted", bufs=3)
            src = x_raw[tower, b, c][:, 2 * h : 2 * h + 2, :]
            nc.vector.tensor_copy(out=x_sorted[job][:], in_=src.rearrange("r i (p u) -> r i u p", u=2))

        def turn_x(job, copy=nc.scalar.copy):
            tower, b, c, h = job
            ps = turn_bank()
            for i in range(2):
                for u in range(2):
                    pairs = x_sorted[job][:, i, u, :] if job in x_sorted else x_raw[tower, b, c][:, 2 * h + i, u::2]
                    nc.tensor.transpose(ps[:, cols(2 * i + u)], pairs, ident[:])
            if h == 0:
                x_grouped[tower, b, c] = work.tile(
                    [P, PACK * ROWS[tower]], BF16, name="x_grouped", tag="x_grouped", bufs=4, align_bytes=64
                )
            copy(
                out=x_grouped[tower, b, c][:].bitcast(F32)[:, span(h)].rearrange("p (i r u) -> p i r u", i=2, u=2),
                in_=ps[:].rearrange("p (i u r) -> p i r u", i=2, u=2),
            )

        def quantize_x(job):
            tower, b, c, h = job
            if tower == "txt" and h == 0:
                return
            shape, bufs = [P, ROWS[tower]], 3 * PASSES[tower]
            codes = work.tile(shape, U32, name="x_codes", tag="x_codes_" + tower, bufs=bufs, align_bytes=64)
            scales = work.tile(shape, U8, name="x_scales", tag="x_scales_" + tower, bufs=bufs, align_bytes=64)
            nc.vector.quantize_mx(out=codes[:].bitcast(FP8X4), scales=scales[:], in_=x_grouped[tower, b, c][:])
            x_codes[tower, b, c], x_scales[tower, b, c] = codes, scales

        def mx_pass(unit, s, c, ps):
            tower, b, g = unit
            xc, xs = x_codes[tower, b, c], x_scales[tower, b, c]
            wc, ws = w_codes[tower][:, c, span(g)], w_scales[tower][:, c, span(g)]
            if tower == "img":
                lhs, lhs_s, rhs, rhs_s = xc[:, cols(s)], xs[:, cols(s)], wc, ws
            else:
                lhs, lhs_s, rhs, rhs_s = wc[:, cols(s)], ws[:, cols(s)], xc[:], xs[:]
            nc.tensor.matmul_mx(
                out=ps[:],
                lhsT=lhs.bitcast(FP8X4),
                lhsT_scale=lhs_s,
                rhs=rhs.bitcast(FP8X4),
                rhs_scale=rhs_s,
                start=(c == 0),
                stop=(c == PASSES[tower] - 1),
            )

        def product(unit, s):
            ps = product_bank()
            for c in range(PASSES[unit[0]]):
                mx_pass(unit, s, c, ps)
            return ps

        def rows_tile(unit):
            y_rows[unit] = work.tile([P, ROWS[unit[0]] // P, SPAN], F32, name="y_rows", tag="y_rows", bufs=4)

        def rows_out(unit):
            tower, b, g = unit
            m0 = first_row[tower] + b * ROWS[tower]
            return out_0[m0 : m0 + ROWS[tower], span(g)].rearrange("(i r) n -> r i n", r=P)

        def add_bias(unit, s, ps):
            if s == 0:
                rows_tile(unit)
            nc.vector.tensor_tensor(out=y_rows[unit][:, s, :], in0=ps[:], in1=bi_rows[:, span(unit[2])], op=ALU.add)

        def squash(unit, t, ps):
            if t == 0:
                v_t[unit] = work.tile([P, PACK, ROWS["txt"]], F32, name="v_t", tag="v_t", bufs=4)
            nc.scalar.activation(out=v_t[unit][:, t, :], in_=ps[:], func=ACT.Tanh, bias=bt[:, unit[2], t : t + 1])

        def gain(r):
            unit = unit_of(r)
            for t in (2 * (r % 2), 2 * (r % 2) + 1):
                v = v_t[unit][:, t, :]
                nc.vector.tensor_scalar(out=v, in0=v, scalar1=gt[:, unit[2], t : t + 1], scalar2=None, op0=ALU.mult)

        def grouped_tile(unit):
            y_grouped[unit] = work.tile(
                [P, PACK * ROWS[unit[0]]], BF16, name="y_grouped", tag="y_grouped", bufs=3, align_bytes=64
            )
            return y_grouped[unit]

        def round_v(unit):
            nc.vector.tensor_copy(
                out=grouped_tile(unit)[:].rearrange("p (a i t) -> p a t i", i=4, t=PACK),
                in_=v_t[unit][:].rearrange("p t (a i) -> p a t i", i=4),
            )

        def pairs_tile(unit):
            u_pairs[unit] = work.tile([P, 2 * SPAN], BF16, name="u_pairs", tag="u_pairs", bufs=3)
            return u_pairs[unit]

        def round_u(unit):
            nc.scalar.copy(
                out=pairs_tile(unit)[:].rearrange("r (i u p e) -> r i p u e", i=2, u=2, e=2),
                in_=y_rows[unit][:].rearrange("r i (p u e) -> r i p u e", u=2, e=2),
            )

        def turn_u(unit):
            ps = turn_bank()
            pairs = u_pairs[unit][:].bitcast(F32)
            for q in range(4):
                nc.tensor.transpose(ps[:, cols(q)], pairs[:, cols(q)], ident[:])
            nc.scalar.copy(
                out=grouped_tile(unit)[:].bitcast(F32).rearrange("p (i r u) -> p i r u", i=2, u=2),
                in_=ps[:].rearrange("p (i u r) -> p i r u", i=2, u=2),
            )

        def turn_v(unit, i):
            ps = turn_bank()
            for t in range(PACK):
                nc.tensor.transpose(ps[:, cols(t)], v_t[unit][:, t, cols(i)], ident[:])
            if i == 0:
                rows_tile(unit)
            nc.scalar.copy(
                out=y_rows[unit][:, i, :].rearrange("r (p t) -> r p t", t=PACK),
                in_=ps[:].rearrange("r (t p) -> r p t", t=PACK),
            )

        def store_scales(tower, queues):
            lo, rows = first_row[tower], y_scales[tower].shape[2]
            for q in range(4):
                queues[q % len(queues)].dma_start(
                    out=scales_out[:, 4 * q : 4 * q + 4, lo // 4 : (lo + rows) // 4].rearrange("g r m -> r g m"),
                    in_=y_scales[tower][32 * q : 32 * q + 4, :, :].bitcast(I32),
                )

        def quantize_y(unit):
            tower, b, g = unit
            rows = ROWS[tower]
            m0 = first_row[tower] + b * rows
            codes = work.tile([P, rows], U32, name="y_codes", tag="y_codes", bufs=4, align_bytes=64)
            nc.vector.quantize_mx(
                out=codes[:].bitcast(FP8X4),
                scales=y_scales[tower][:, g, b * rows : (b + 1) * rows],
                in_=y_grouped[unit][:],
            )
            nc.sync.dma_start(out=words_out[g, :, m0 : m0 + rows], in_=codes[:].bitcast(I32))

        def spread_bias():
            ps = turn_bank()
            pairs = bi[:].rearrange("p g t -> p (g t)").bitcast(F32)
            for q in range(4):
                nc.tensor.transpose(ps[:, cols(q)], pairs[:, q : q + 1].to_broadcast([P, P]), ident[:])
            nc.scalar.copy(
                out=bi_rows[:].bitcast(F32).rearrange("r (g p u) -> r g p u", g=HALVES, u=2),
                in_=ps[:].rearrange("r (g u p) -> r g p u", g=HALVES, u=2),
            )

        loads = []
        for r in range(ROUNDS):
            loads += [("w", w_plan[r])] if r in w_plan else []
            loads += [("x", job) for job in x_plan[r] if job[2:] == (0, 0)]
        free = {"x": RAW_X_TILES - 4, "w": RAW_W_TILES - 2}

        def issue_loads():
            while loads and free[loads[0][0]] > 0:
                kind, job = loads[0]
                loads.remove(loads[0])
                free[kind] -= 1
                if kind == "w":
                    load_w(job)
                else:
                    load_x(job[0], job[1], 0, PASSES[job[0]])

        zeros = work.tile([P, SPAN], BF16, name="zeros", tag="w_grouped", bufs=3, align_bytes=64)
        warm_codes = keep.tile([P, P], U32, name="warm_codes", align_bytes=64)
        warm_scales = keep.tile([P, P], U8, name="warm_scales", align_bytes=64)
        nc.vector.memset(zeros[:], 0.0)
        nc.vector.quantize_mx(out=warm_codes[:].bitcast(FP8X4), scales=warm_scales[:], in_=zeros[:])

        def warm_up(n):
            ps = turn_bank()
            for k in range(n):
                nc.tensor.matmul_mx(
                    out=ps[:, :P],
                    lhsT=warm_codes[:].bitcast(FP8X4),
                    lhsT_scale=warm_scales[:],
                    rhs=warm_codes[:].bitcast(FP8X4),
                    rhs_scale=warm_scales[:],
                    start=True,
                    stop=True,
                )

        load_vector(bi, b_image)
        load_x("txt", 0, 0, 1)
        load_w(("txt", 0, 0))
        load_x("txt", 0, 1, 2)
        load_x("txt", 1, 0, 1)
        load_w(("txt", 1, 0))
        load_x("txt", 1, 1, 2)
        load_vector(bt, b_text)
        load_vector(gt, g_text)
        issue_loads()
        warm_up(WARM_UP[0])
        spread_bias()
        turn_x(("txt", 0, 0, 0))
        turn_x(("txt", 0, 0, 1), nc.vector.tensor_copy)
        group_w_shared(("txt", 0, 0))
        quantize_x(("txt", 0, 0, 1))
        quantize_w(("txt", 0, 0))
        warm_up(WARM_UP[1])
        turn_x(("txt", 0, 1, 0))
        turn_x(("txt", 0, 1, 1))
        warm_up(WARM_UP[2])
        first = [product_bank() if t < PRODUCT_BANKS else turn_bank() for t in range(PACK)]
        for t in range(PACK):
            mx_pass(unit_of(0), t, 0, first[t])
        quantize_x(("txt", 0, 1, 1))
        group_w_shared(("txt", 1, 0))
        turn_x(("txt", 1, 0, 0))
        quantize_w(("txt", 1, 0))
        turn_x(("txt", 1, 0, 1))
        group_w(w_plan[1], nc.vector.tensor_copy, 0, SPAN)
        turn_x(("txt", 1, 1, 0))
        quantize_x(("txt", 1, 0, 1))
        turn_x(("txt", 1, 1, 1))
        free["x"] += 4
        free["w"] += 3
        issue_loads()
        for t in range(PACK):
            mx_pass(unit_of(0), t, 1, first[t])
        for t in range(PACK):
            squash(unit_of(0), t, first[t])
        quantize_x(("txt", 1, 1, 1))
        gain(0)
        quantize_w(w_plan[1])

        last = ROUNDS - 1
        for r in range(2, last):
            unit = unit_of(r)

            if r - 1 < TEXT_ROUNDS:
                gain(r - 1)
            if ended("img", r - 1):
                round_u(ended("img", r - 1))
            if r > 2 and r - 1 in w_plan:
                quantize_w(w_plan[r - 1])
            if ended("txt", r - 3):
                quantize_y(ended("txt", r - 3))
            if r - 3 == TEXT_ROUNDS - 1:
                store_scales("txt", [nc.sync])
            if ended("img", r - 3):
                quantize_y(ended("img", r - 3))
            if ended("txt", r - 2):
                round_v(ended("txt", r - 2))
            if r in w_plan:
                group_w(w_plan[r], nc.vector.tensor_copy, 0, SPAN)

            if r < TEXT_ROUNDS:
                for t in (2 * (r % 2), 2 * (r % 2) + 1):
                    squash(unit, t, product(unit, t))
                for job in x_plan[r - 1]:
                    quantize_x(job)
            else:
                add_bias(unit, 0, product(unit, 0))
                for job in x_plan[r - 1]:
                    quantize_x(job)
                add_bias(unit, 1, product(unit, 1))
                nc.sync.dma_start(out=rows_out(unit), in_=y_rows[unit][:])
                for job in x_plan[r + 1]:
                    sort_x(job)

            for job in x_plan[r]:
                turn_x(job)
                if job[2:] == ((PASSES["img"] - 1, 0) if job[0] == "img" else (PASSES["txt"] - 1, 1)):
                    free["x"] += 1
            if ended("img", r - 2):
                turn_u(ended("img", r - 2))
            for pair in range(2):
                source = ended("txt", r - 2 - pair)
                if source:
                    turn_v(source, 2 * pair)
                    turn_v(source, 2 * pair + 1)
                if source and pair == 1:
                    nc.sync.dma_start(out=rows_out(source), in_=y_rows[source][:])
            if r in w_plan:
                free["w"] += 1
            issue_loads()

        unit = unit_of(last)
        turn_u(unit_of(last - 2))
        round_u(unit_of(last - 1))
        quantize_y(unit_of(last - 3))
        pairs, grouped = pairs_tile(unit)[:], grouped_tile(unit)[:].bitcast(F32)
        quantize_y(unit_of(last - 2))
        for s in range(2):
            ps = product(unit, s)
            nc.vector.tensor_tensor(
                out=pairs[:, span(s)].rearrange("r (u p e) -> r u p e", u=2, e=2),
                in0=ps[:].rearrange("r (p u e) -> r u p e", u=2, e=2),
                in1=bi_rows[:, span(unit[2])].rearrange("r (p u e) -> r u p e", u=2, e=2),
                op=ALU.add,
            )
            add_bias(unit, s, ps)
            nc.sync.dma_start(out=rows_out(unit)[:, s, :], in_=y_rows[unit][:, s, :])
        turn_u(unit_of(last - 1))
        for s in range(2):
            ps = turn_bank()
            for u in range(2):
                nc.tensor.transpose(ps[:, cols(u)], pairs.bitcast(F32)[:, cols(2 * s + u)], ident[:])
            nc.scalar.copy(
                out=grouped[:, 2 * s * P : 2 * (s + 1) * P].rearrange("p (r u) -> p r u", u=2),
                in_=ps[:, : 2 * P].rearrange("p (u r) -> p r u", u=2),
            )
        quantize_y(unit_of(last - 1))
        quantize_y(unit)
        store_scales("img", [nc.sync, nc.scalar])
